import numpy as np
import ml_dtypes


def mxq(x, axis, fmt="e4m3"):
    dtype, down = {"e4m3": (ml_dtypes.float8_e4m3fn, 7), "e5m2": (ml_dtypes.float8_e5m2, 14)}[fmt]
    v = np.moveaxis(np.asarray(x, np.float32).astype(ml_dtypes.bfloat16).astype(np.float64), axis, -1)
    blocks = v.reshape(v.shape[:-1] + (-1, 32))
    amax = np.abs(blocks).max(-1, keepdims=True)
    byte = np.maximum(np.where(amax > 0, np.frexp(amax)[1] - 1 + 127, 0) - down, 1)
    scale = np.exp2(byte - 127.0)
    codes = (blocks / scale).astype(np.float32).astype(dtype).astype(np.float64)
    return np.moveaxis((codes * scale).reshape(v.shape), -1, axis)


WIDE = False


def mx_kscale(k):
    if not WIDE:
        return np.ones(k)
    levels = np.array([10, -10, 5, -5, 0])
    if k % 512:
        return np.exp2(np.random.permutation(np.resize(levels, k // 32))).repeat(32)
    a = np.empty((k // 512, 16))
    for p in range(k // 512):
        a[p, :8] = np.random.permutation(np.resize(levels, 8))
        for g in range(8):
            far = levels[np.abs(levels - a[p, g]) >= 10]
            a[p, g + 8] = far[np.random.randint(len(far))]
    return np.exp2(a.ravel()).repeat(32)


def f64(x):
    return np.asarray(x).astype(np.float64)


def striped(idx):
    return np.tile(np.asarray(idx).reshape(-1, 16).T, (8, 1)).astype(np.uint16)


def unstriped(offs):
    return offs[:16].T.reshape(-1).astype(np.int64)


B, N, T, D, DV, NQ = 2, 512, 2048, 512, 512, 128
PAGE = 64


def setup_inputs():
    n = np.random.standard_normal
    pages = np.random.permutation(T // PAGE)[:B * N // PAGE]
    idx = (pages[:, None] * PAGE + np.arange(PAGE)[None, :]).reshape(-1)
    s = mx_kscale(D)[:, None]
    u = np.ones(T)
    u[idx] = mx_kscale(B * N)
    r = np.random.uniform(0.5, 2.0, T)
    k = n((D, T)) / s
    v = n((DV, T)) / (u * r)
    return {
        "qT": (n((B, D, NQ)) * s * (0.80 / np.sqrt(D))).astype(np.float32),
        "kT": k.astype(np.float32),
        "vT": v.astype(np.float32),
        "vs": np.tile(u * r, (128, 1)).astype(np.float32),
        "og": n((B, NQ, DV)).astype(np.float32),
        "offs": striped(idx),
    }


def reference(qT, kT, vT, vs, og, offs):
    idx = unstriped(offs)
    k = f64(kT)
    v = f64(vT)
    pick = lambda x: x[:, idx].reshape(x.shape[0], B, N).transpose(1, 0, 2)
    q = f64(qT)
    score = mxq(q, 1, "e4m3").transpose(0, 2, 1) @ mxq(pick(k), 1, "e4m3")
    m = score.max(-1, keepdims=True)
    p = np.exp(score - m)
    total = p.sum(-1, keepdims=True)
    w = p * pick(f64(vs))[:, :1, :]
    y = mxq(w, 2, "e4m3") @ mxq(pick(v).transpose(0, 2, 1), 1, "e4m3")
    y = y / total
    y = y / (1.0 + np.exp(-f64(og)))
    return y

@@ -1,0 +1,241 @@
+from contextlib import ExitStack
+
+import concourse.mybir as mybir
+from concourse.masks import make_identity
+
+B, N, T, D, DV, NQ = 2, 512, 2048, 512, 512, 128
+FLOPS = 2 * B * NQ * N * (D + DV)
+
+P = 128
+PACK = 4
+EB = DV // P
+
+F32 = mybir.dt.float32
+BF16 = mybir.dt.bfloat16
+U32 = mybir.dt.uint32
+U16 = mybir.dt.uint16
+U8 = mybir.dt.uint8
+FP8X4 = mybir.dt.float8_e4m3fn_x4
+ACT = mybir.ActivationFunctionType
+ALU = mybir.AluOpType
+AXIS = mybir.AxisListType
+
+
+def tile_attend_gate_kernel(tc, qT, kT, vT, vs, og, offs, out):
+    nc = tc.nc
+    with ExitStack() as ctx:
+        keep = ctx.enter_context(tc.tile_pool(name="keep", bufs=1))
+        psum = ctx.enter_context(tc.psum_pool(name="psum", bufs=1))
+
+        lists = keep.tile([P, B * N // 16], U16, name="lists")
+        nc.sync.dma_start(lists[:], offs)
+        k_rows = kT.rearrange("(p j) t -> p j t", j=PACK)
+        k_pool = [keep.tile([P, T], F32, name=f"k_pool{j}") for j in range(PACK)]
+        v_pool = [keep.tile([P, T], F32, name=f"v_pool{e}") for e in range(EB)]
+        scale_pool = keep.tile([P, T], F32, name="scale_pool")
+        nc.vector.memset(scale_pool[:], 0.0)
+        nc.sync.dma_start(k_pool[0][:], k_rows[:, 0, :])
+        nc.sync.dma_start(scale_pool[0:1, :], vs[0:1, :])
+        for j in range(1, PACK):
+            nc.sync.dma_start(k_pool[j][:], k_rows[:, j, :])
+        q_raw = keep.tile([P, B, PACK, NQ], F32, name="q_raw")
+        nc.sync.dma_start(q_raw[:], qT.rearrange("b (p j) q -> p b j q", j=PACK))
+        gates = [keep.tile([P, B, DV // 2], F32, name=f"gate{h}") for h in range(2)]
+        gate_rows = og.rearrange("b q e -> q b e")
+        for e in range(EB):
+            if e == EB - 1:
+                nc.sync.dma_start(gates[0][:], gate_rows[:, :, : DV // 2])
+            nc.sync.dma_start(v_pool[e][:], vT[e * P : (e + 1) * P, :])
+        nc.sync.dma_start(gates[1][:], gate_rows[:, :, DV // 2 :])
+
+        warm = keep.tile([P, 1], F32, name="warm")
+        nc.gpsimd.memset(warm[:], 0.0)
+        nc.scalar.activation(warm[:], warm[:], ACT.Exp)
+        ident_f = keep.tile([P, P], F32, name="ident_f")
+        make_identity(nc, ident_f[:])
+        ident_b = keep.tile([P, P], BF16, name="ident_b")
+        make_identity(nc, ident_b[:])
+
+        vs_row = keep.tile([P, B * N], F32, name="vs_row")
+        nc.vector.tensor_copy(vs_row[:], scale_pool[:].indirect(lists[:]))
+        vs_col = []
+        for b in range(B):
+            turned = psum.tile([P, PACK, P], F32, tag="wide", bufs=3, name="turned")
+            for t in range(PACK):
+                nc.tensor.transpose(turned[:, t, :], vs_row[:, b * N + t : (b + 1) * N : PACK], ident_f[:])
+            col = keep.tile([P, PACK], F32, name=f"vs_col{b}")
+            nc.scalar.copy(col[:], turned[:, :, 0])
+            vs_col.append(col)
+
+        k_got = keep.tile([P, PACK, B * N], F32, name="k_got")
+        k_bf = keep.tile([P, B * N, PACK], BF16, align_bytes=64, name="k_bf")
+        k_codes = keep.tile([P, B * N], U32, align_bytes=64, name="k_codes")
+        k_scales = keep.tile([P, B * N], U8, align_bytes=64, name="k_scales")
+        for j in range(PACK):
+            if j < PACK - 1:
+                nc.vector.tensor_copy(k_got[:, j, :], k_pool[j][:].indirect(lists[:]))
+            else:
+                for b in range(B):
+                    nc.vector.tensor_copy(
+                        k_got[:, j, b * N : (b + 1) * N],
+                        k_pool[j][:].indirect(lists[:, b * N // 16 : (b + 1) * N // 16]),
+                    )
+
+        def interleave_keys(copy, first, last):
+            copy(
+                k_bf[:, first:last, :].rearrange("p (c i) t -> p c t i", i=4),
+                k_got[:, :, first:last].rearrange("p t (c i) -> p c t i", i=4),
+            )
+
+        for b in range(B):
+            interleave_keys(nc.scalar.copy, b * N, b * N + N // 2)
+            interleave_keys(nc.vector.tensor_copy, b * N + N // 2, (b + 1) * N)
+
+        q_bf = keep.tile([P, B, NQ, PACK], BF16, align_bytes=64, name="q_bf")
+        q_codes = keep.tile([P, B * NQ], U32, align_bytes=64, name="q_codes")
+        q_scales = keep.tile([P, B * NQ], U8, align_bytes=64, name="q_scales")
+        nc.vector.tensor_copy(q_bf[:], q_raw[:].rearrange("p b j q -> p b q j"))
+        nc.vector.quantize_mx(
+            out=q_codes[:].bitcast(FP8X4), scales=q_scales[:], in_=q_bf[:].rearrange("p b q j -> p (b q j)")
+        )
+
+        top = [keep.tile([P, 1], F32, name=f"top{b}") for b in range(B)]
+        minus = [keep.tile([P, 1], F32, name=f"minus{b}") for b in range(B)]
+        total = [keep.tile([P, 1], F32, name=f"total{b}") for b in range(B)]
+        half = [keep.tile([P, 1], F32, name=f"half{b}") for b in range(B)]
+        weight = [keep.tile([P, PACK, P], F32, name=f"weight{b}") for b in range(B)]
+        w_bf = [keep.tile([P, NQ, PACK], BF16, align_bytes=64, name=f"w_bf{b}") for b in range(B)]
+        w_codes = [keep.tile([P, NQ], U32, align_bytes=64, name=f"w_codes{b}") for b in range(B)]
+        w_scales = [keep.tile([P, NQ], U8, align_bytes=64, name=f"w_scales{b}") for b in range(B)]
+
+        def scores(b):
+            s = slice(b * N, (b + 1) * N)
+            qs = slice(b * NQ, (b + 1) * NQ)
+            nc.vector.quantize_mx(
+                out=k_codes[:, s].bitcast(FP8X4), scales=k_scales[:, s], in_=k_bf[:, s, :].rearrange("p n t -> p (n t)")
+            )
+            score = psum.tile([P, N], F32, tag="wide", bufs=3, name="score")
+            nc.tensor.matmul_mx(
+                out=score[:],
+                lhsT=q_codes[:, qs].bitcast(FP8X4),
+                lhsT_scale=q_scales[:, qs],
+                rhs=k_codes[:, s].bitcast(FP8X4),
+                rhs_scale=k_scales[:, s],
+                start=True,
+                stop=True,
+            )
+            return score
+
+        def softmax(b, score):
+            nc.vector.reduce_max(top[b][:], score[:], axis=AXIS.X)
+            nc.scalar.mul(minus[b][:], top[b][:], -1.0)
+            nc.scalar.activation(
+                weight[b][:],
+                score[:].rearrange("p (c t) -> p t c", t=PACK),
+                ACT.Exp,
+                bias=minus[b][:],
+                accum_out=total[b][:],
+            )
+
+        def weights(b):
+            turned = psum.tile([P, PACK, P], F32, tag="wide", bufs=3, name="turned")
+            for t in range(PACK):
+                nc.tensor.transpose(turned[:, t, :], weight[b][:, t, :], ident_f[:])
+            nc.vector.tensor_tensor(
+                w_bf[b][:],
+                turned[:].rearrange("p t q -> p q t"),
+                vs_col[b][:].unsqueeze(1).to_broadcast([P, NQ, PACK]),
+                ALU.mult,
+            )
+            nc.vector.quantize_mx(
+                out=w_codes[b][:].bitcast(FP8X4), scales=w_scales[b][:], in_=w_bf[b][:].rearrange("p q t -> p (q t)")
+            )
+            nc.vector.reciprocal(half[b][:], total[b][:])
+            nc.vector.tensor_scalar_mul(half[b][:], half[b][:], 0.5)
+
+        v_got = [keep.tile([P, B, PACK, P], BF16, name=f"v_got{e}") for e in range(EB)]
+        v_bf = [keep.tile([P, B, P, PACK], BF16, align_bytes=64, name=f"v_bf{e}") for e in range(EB)]
+        v_codes = [keep.tile([P, B * P], U32, align_bytes=64, name=f"v_codes{e}") for e in range(EB)]
+        v_scales = [keep.tile([P, B * P], U8, align_bytes=64, name=f"v_scales{e}") for e in range(EB)]
+
+        def gather_values(e, split):
+            if split:
+                for b in range(B):
+                    nc.vector.tensor_copy(
+                        v_got[e][:, b, :, :].rearrange("p t c -> p c t"),
+                        v_pool[e][:].indirect(lists[:, b * N // 16 : (b + 1) * N // 16]),
+                    )
+            else:
+                nc.vector.tensor_copy(v_got[e][:].rearrange("p b t c -> p b c t"), v_pool[e][:].indirect(lists[:]))
+            for b in range(B):
+                turned_v = psum.tile([P, PACK, P], BF16, tag="values", bufs=3, name="turned_v")
+                for t in range(PACK):
+                    nc.tensor.transpose(turned_v[:, t, :], v_got[e][:, b, t, :], ident_b[:])
+                nc.scalar.copy(v_bf[e][:, b, :, :], turned_v[:].rearrange("p t e -> p e t"))
+
+        def quantize_values(e, first, last):
+            cols = slice(first * P, last * P)
+            nc.vector.quantize_mx(
+                out=v_codes[e][:, cols].bitcast(FP8X4),
+                scales=v_scales[e][:, cols],
+                in_=v_bf[e][:, first:last, :, :].rearrange("p b e t -> p (b e t)"),
+            )
+
+        tanh = [keep.tile([P, B, DV // 2], F32, name=f"tanh{h}") for h in range(2)]
+        factor = keep.tile([P, B, DV], F32, name="factor")
+
+        def gate_factor(h):
+            nc.scalar.activation(tanh[h][:], gates[h][:], ACT.Tanh, scale=0.5)
+            for b in range(B):
+                nc.vector.tensor_scalar(
+                    factor[:, b, h * (DV // 2) : (h + 1) * (DV // 2)], tanh[h][:, b, :], 1.0, half[b][:], ALU.add, ALU.mult
+                )
+
+        res = keep.tile([P, B, DV], F32, name="res")
+
+        def attend(e):
+            y = psum.tile([P, B, P], F32, tag="y", bufs=2, name="y")
+            es = slice(e * P, (e + 1) * P)
+            for b in range(B):
+                cols = slice(b * P, (b + 1) * P)
+                nc.tensor.matmul_mx(
+                    out=y[:, b, :],
+                    lhsT=w_codes[b][:].bitcast(FP8X4),
+                    lhsT_scale=w_scales[b][:],
+                    rhs=v_codes[e][:, cols].bitcast(FP8X4),
+                    rhs_scale=v_scales[e][:, cols],
+                    start=True,
+                    stop=True,
+                )
+            nc.vector.tensor_tensor(res[:, :, es], y[:], factor[:, :, es], ALU.mult)
+
+        out_rows = out.rearrange("b q e -> q b e")
+
+        def store(first, last):
+            es = slice(first * P, last * P)
+            nc.sync.dma_start(out_rows[:, :, es], res[:, :, es])
+
+        score0 = scores(0)
+        score1 = scores(1)
+        softmax(0, score0)
+        gather_values(0, False)
+        softmax(1, score1)
+        weights(0)
+        gather_values(1, False)
+        weights(1)
+        quantize_values(0, 0, 2)
+        gather_values(2, False)
+        quantize_values(1, 0, 2)
+        gate_factor(0)
+        attend(0)
+        attend(1)
+        store(0, 2)
+        quantize_values(2, 0, 2)
+        gather_values(3, True)
+        gate_factor(1)
+        attend(2)
+        store(2, 3)
+        quantize_values(3, 0, 1)
+        quantize_values(3, 1, 2)
+        attend(3)
+        store(3, 4)

@@ -20,6 +20,9 @@ ACT = mybir.ActivationFunctionType
 ALU = mybir.AluOpType
 AXIS = mybir.AxisListType
 
+KEY_CHUNK = 1024
+SCALAR_SHARE = [1024, 512, 512, 352]
+
 
 def tile_attend_gate_kernel(tc, qT, kT, vT, vs, og, offs, out):
     nc = tc.nc
@@ -29,92 +32,97 @@ def tile_attend_gate_kernel(tc, qT, kT, vT, vs, og, offs, out):
 
         lists = keep.tile([P, B * N // 16], U16, name="lists")
         nc.sync.dma_start(lists[:], offs)
-        k_rows = kT.rearrange("(p j) t -> p j t", j=PACK)
-        k_pool = [keep.tile([P, T], F32, name=f"k_pool{j}") for j in range(PACK)]
-        v_pool = [keep.tile([P, T], F32, name=f"v_pool{e}") for e in range(EB)]
-        scale_pool = keep.tile([P, T], F32, name="scale_pool")
-        nc.vector.memset(scale_pool[:], 0.0)
-        nc.sync.dma_start(k_pool[0][:], k_rows[:, 0, :])
-        nc.sync.dma_start(scale_pool[0:1, :], vs[0:1, :])
-        for j in range(1, PACK):
-            nc.sync.dma_start(k_pool[j][:], k_rows[:, j, :])
+        scale_row = keep.tile([1, T], F32, name="scale_row")
+        nc.sync.dma_start(scale_row[:], vs[0:1, :])
+        k_rows = kT.rearrange("(p a h) t -> p a h t", a=2, h=2)
+        k_raw = []
+        for a in range(2):
+            for c in range(T // KEY_CHUNK):
+                raw = keep.tile([P, 2, KEY_CHUNK], F32, name=f"k_raw{a}{c}")
+                nc.sync.dma_start(raw[:], k_rows[:, a, :, c * KEY_CHUNK : (c + 1) * KEY_CHUNK])
+                k_raw.append(raw)
         q_raw = keep.tile([P, B, PACK, NQ], F32, name="q_raw")
         nc.sync.dma_start(q_raw[:], qT.rearrange("b (p j) q -> p b j q", j=PACK))
-        gates = [keep.tile([P, B, DV // 2], F32, name=f"gate{h}") for h in range(2)]
-        gate_rows = og.rearrange("b q e -> q b e")
+        v_pool = [keep.tile([P, T], F32, name=f"v_pool{e}") for e in range(EB)]
+        gate = keep.tile([P, B, DV], F32, name="gate")
         for e in range(EB):
-            if e == EB - 1:
-                nc.sync.dma_start(gates[0][:], gate_rows[:, :, : DV // 2])
+            if e == 2:
+                nc.sync.dma_start(gate[:], og.rearrange("b q e -> q b e"))
             nc.sync.dma_start(v_pool[e][:], vT[e * P : (e + 1) * P, :])
-        nc.sync.dma_start(gates[1][:], gate_rows[:, :, DV // 2 :])
 
         warm = keep.tile([P, 1], F32, name="warm")
         nc.gpsimd.memset(warm[:], 0.0)
         nc.scalar.activation(warm[:], warm[:], ACT.Exp)
-        ident_f = keep.tile([P, P], F32, name="ident_f")
-        make_identity(nc, ident_f[:])
-        ident_b = keep.tile([P, P], BF16, name="ident_b")
-        make_identity(nc, ident_b[:])
+        ident = keep.tile([P, P], F32, name="ident")
+        make_identity(nc, ident[:])
 
+        scale_pool = keep.tile([P, T], F32, name="scale_pool")
+        nc.vector.memset(scale_pool[:], 0.0)
+        nc.vector.tensor_copy(scale_pool[0:1, :], scale_row[:])
         vs_row = keep.tile([P, B * N], F32, name="vs_row")
         nc.vector.tensor_copy(vs_row[:], scale_pool[:].indirect(lists[:]))
         vs_col = []
         for b in range(B):
-            turned = psum.tile([P, PACK, P], F32, tag="wide", bufs=3, name="turned")
+            turned = psum.tile([P, PACK, P], F32, tag="wide", bufs=4, name="turned")
             for t in range(PACK):
-                nc.tensor.transpose(turned[:, t, :], vs_row[:, b * N + t : (b + 1) * N : PACK], ident_f[:])
+                nc.tensor.transpose(turned[:, t, :], vs_row[:, b * N + t : (b + 1) * N : PACK], ident[:])
             col = keep.tile([P, PACK], F32, name=f"vs_col{b}")
             nc.scalar.copy(col[:], turned[:, :, 0])
             vs_col.append(col)
 
-        k_got = keep.tile([P, PACK, B * N], F32, name="k_got")
-        k_bf = keep.tile([P, B * N, PACK], BF16, align_bytes=64, name="k_bf")
+        k_pair = [keep.tile([P, T, 2], BF16, name=f"k_pair{a}") for a in range(2)]
+        k_got = keep.tile([P, 2, B * N], U32, name="k_got")
+        k_words = keep.tile([P, B * N, 2], U32, align_bytes=64, name="k_words")
         k_codes = keep.tile([P, B * N], U32, align_bytes=64, name="k_codes")
         k_scales = keep.tile([P, B * N], U8, align_bytes=64, name="k_scales")
-        for j in range(PACK):
-            if j < PACK - 1:
-                nc.vector.tensor_copy(k_got[:, j, :], k_pool[j][:].indirect(lists[:]))
+        for a in range(2):
+            for c in range(T // KEY_CHUNK):
+                i = a * (T // KEY_CHUNK) + c
+                src = k_raw[i][:].rearrange("p h t -> p t h")
+                first = c * KEY_CHUNK
+                cut = SCALAR_SHARE[i]
+                nc.scalar.activation(k_pair[a][:, first : first + cut, :], src[:, :cut, :], ACT.Copy)
+                if cut < KEY_CHUNK:
+                    nc.vector.tensor_copy(k_pair[a][:, first + cut : first + KEY_CHUNK, :], src[:, cut:, :])
+            window = k_pair[a][:].rearrange("p t h -> p (t h)").bitcast(U32)
+            if a == 0:
+                nc.vector.tensor_copy(k_got[:, a, :], window.indirect(lists[:]))
             else:
                 for b in range(B):
                     nc.vector.tensor_copy(
-                        k_got[:, j, b * N : (b + 1) * N],
-                        k_pool[j][:].indirect(lists[:, b * N // 16 : (b + 1) * N // 16]),
+                        k_got[:, a, b * N : (b + 1) * N], window.indirect(lists[:, b * N // 16 : (b + 1) * N // 16])
                     )
-
-        def interleave_keys(copy, first, last):
-            copy(
-                k_bf[:, first:last, :].rearrange("p (c i) t -> p c t i", i=4),
-                k_got[:, :, first:last].rearrange("p t (c i) -> p c t i", i=4),
-            )
-
-        for b in range(B):
-            interleave_keys(nc.scalar.copy, b * N, b * N + N // 2)
-            interleave_keys(nc.vector.tensor_copy, b * N + N // 2, (b + 1) * N)
 
         q_bf = keep.tile([P, B, NQ, PACK], BF16, align_bytes=64, name="q_bf")
         q_codes = keep.tile([P, B * NQ], U32, align_bytes=64, name="q_codes")
         q_scales = keep.tile([P, B * NQ], U8, align_bytes=64, name="q_scales")
-        nc.vector.tensor_copy(q_bf[:], q_raw[:].rearrange("p b j q -> p b q j"))
+        nc.scalar.copy(
+            q_bf[:].rearrange("p b (c i) j -> p b c j i", i=4),
+            q_raw[:].rearrange("p b j (c i) -> p b c j i", i=4),
+        )
         nc.vector.quantize_mx(
             out=q_codes[:].bitcast(FP8X4), scales=q_scales[:], in_=q_bf[:].rearrange("p b q j -> p (b q j)")
         )
 
-        top = [keep.tile([P, 1], F32, name=f"top{b}") for b in range(B)]
         minus = [keep.tile([P, 1], F32, name=f"minus{b}") for b in range(B)]
-        total = [keep.tile([P, 1], F32, name=f"total{b}") for b in range(B)]
-        half = [keep.tile([P, 1], F32, name=f"half{b}") for b in range(B)]
+        total = keep.tile([P, B], F32, name="total")
+        twice = keep.tile([P, B], F32, name="twice")
+        half = keep.tile([P, B], F32, name="half")
         weight = [keep.tile([P, PACK, P], F32, name=f"weight{b}") for b in range(B)]
-        w_bf = [keep.tile([P, NQ, PACK], BF16, align_bytes=64, name=f"w_bf{b}") for b in range(B)]
-        w_codes = [keep.tile([P, NQ], U32, align_bytes=64, name=f"w_codes{b}") for b in range(B)]
-        w_scales = [keep.tile([P, NQ], U8, align_bytes=64, name=f"w_scales{b}") for b in range(B)]
+        w_bf = keep.tile([P, B, NQ, PACK], BF16, align_bytes=64, name="w_bf")
+        w_codes = keep.tile([P, B * NQ], U32, align_bytes=64, name="w_codes")
+        w_scales = keep.tile([P, B * NQ], U8, align_bytes=64, name="w_scales")
 
         def scores(b):
             s = slice(b * N, (b + 1) * N)
             qs = slice(b * NQ, (b + 1) * NQ)
+            nc.scalar.copy(k_words[:, s, :], k_got[:, :, s].rearrange("p a n -> p n a"))
             nc.vector.quantize_mx(
-                out=k_codes[:, s].bitcast(FP8X4), scales=k_scales[:, s], in_=k_bf[:, s, :].rearrange("p n t -> p (n t)")
+                out=k_codes[:, s].bitcast(FP8X4),
+                scales=k_scales[:, s],
+                in_=k_words[:, s, :].rearrange("p n a -> p (n a)").bitcast(BF16),
             )
-            score = psum.tile([P, N], F32, tag="wide", bufs=3, name="score")
+            score = psum.tile([P, N], F32, tag="wide", bufs=4, name="score")
             nc.tensor.matmul_mx(
                 out=score[:],
                 lhsT=q_codes[:, qs].bitcast(FP8X4),
@@ -127,115 +135,111 @@ def tile_attend_gate_kernel(tc, qT, kT, vT, vs, og, offs, out):
             return score
 
         def softmax(b, score):
-            nc.vector.reduce_max(top[b][:], score[:], axis=AXIS.X)
-            nc.scalar.mul(minus[b][:], top[b][:], -1.0)
+            nc.vector.tensor_reduce(minus[b][:], score[:], axis=AXIS.X, op=ALU.max, negate=True)
             nc.scalar.activation(
                 weight[b][:],
                 score[:].rearrange("p (c t) -> p t c", t=PACK),
                 ACT.Exp,
                 bias=minus[b][:],
-                accum_out=total[b][:],
+                accum_out=total[:, b : b + 1],
             )
 
         def weights(b):
-            turned = psum.tile([P, PACK, P], F32, tag="wide", bufs=3, name="turned")
+            qs = slice(b * NQ, (b + 1) * NQ)
+            turned = psum.tile([P, PACK, P], F32, tag="wide", bufs=4, name="turned")
             for t in range(PACK):
-                nc.tensor.transpose(turned[:, t, :], weight[b][:, t, :], ident_f[:])
+                nc.tensor.transpose(turned[:, t, :], weight[b][:, t, :], ident[:])
             nc.vector.tensor_tensor(
-                w_bf[b][:],
+                w_bf[:, b, :, :],
                 turned[:].rearrange("p t q -> p q t"),
                 vs_col[b][:].unsqueeze(1).to_broadcast([P, NQ, PACK]),
                 ALU.mult,
             )
-            nc.vector.quantize_mx(
-                out=w_codes[b][:].bitcast(FP8X4), scales=w_scales[b][:], in_=w_bf[b][:].rearrange("p q t -> p (q t)")
-            )
-            nc.vector.reciprocal(half[b][:], total[b][:])
-            nc.vector.tensor_scalar_mul(half[b][:], half[b][:], 0.5)
 
-        v_got = [keep.tile([P, B, PACK, P], BF16, name=f"v_got{e}") for e in range(EB)]
-        v_bf = [keep.tile([P, B, P, PACK], BF16, align_bytes=64, name=f"v_bf{e}") for e in range(EB)]
+        def quantize_weights():
+            nc.vector.quantize_mx(
+                out=w_codes[:].bitcast(FP8X4), scales=w_scales[:], in_=w_bf[:].rearrange("p b q t -> p (b q t)")
+            )
+
+        v_got = [keep.tile([P, 2, B * P, 2], BF16, name=f"v_got{e}") for e in range(EB)]
+        v_words = [keep.tile([P, B, P, 2], F32, align_bytes=64, name=f"v_words{e}") for e in range(EB)]
         v_codes = [keep.tile([P, B * P], U32, align_bytes=64, name=f"v_codes{e}") for e in range(EB)]
         v_scales = [keep.tile([P, B * P], U8, align_bytes=64, name=f"v_scales{e}") for e in range(EB)]
 
-        def gather_values(e, split):
-            if split:
-                for b in range(B):
-                    nc.vector.tensor_copy(
-                        v_got[e][:, b, :, :].rearrange("p t c -> p c t"),
-                        v_pool[e][:].indirect(lists[:, b * N // 16 : (b + 1) * N // 16]),
-                    )
-            else:
-                nc.vector.tensor_copy(v_got[e][:].rearrange("p b t c -> p b c t"), v_pool[e][:].indirect(lists[:]))
-            for b in range(B):
-                turned_v = psum.tile([P, PACK, P], BF16, tag="values", bufs=3, name="turned_v")
-                for t in range(PACK):
-                    nc.tensor.transpose(turned_v[:, t, :], v_got[e][:, b, t, :], ident_b[:])
-                nc.scalar.copy(v_bf[e][:, b, :, :], turned_v[:].rearrange("p t e -> p e t"))
+        def gather_values(e, first, last):
+            nc.vector.tensor_copy(
+                v_got[e][:, :, first * P : last * P, :].rearrange("p u c h -> p c u h"),
+                v_pool[e][:].indirect(lists[:, first * N // 16 : last * N // 16]),
+            )
+            words = v_got[e][:].rearrange("p u c h -> p u (c h)").bitcast(F32)
+            turned_v = psum.tile([P, B, 2, P], F32, tag="values", bufs=2, name="turned_v")
+            for b in range(first, last):
+                for u in range(2):
+                    nc.tensor.transpose(turned_v[:, b, u, :], words[:, u, b * P : (b + 1) * P], ident[:])
+            nc.scalar.copy(
+                v_words[e][:, first:last, :, :], turned_v[:, first:last, :, :].rearrange("p b u e -> p b e u")
+            )
 
         def quantize_values(e, first, last):
             cols = slice(first * P, last * P)
             nc.vector.quantize_mx(
                 out=v_codes[e][:, cols].bitcast(FP8X4),
                 scales=v_scales[e][:, cols],
-                in_=v_bf[e][:, first:last, :, :].rearrange("p b e t -> p (b e t)"),
+                in_=v_words[e][:, first:last, :, :].rearrange("p b e u -> p (b e u)").bitcast(BF16),
             )
 
-        tanh = [keep.tile([P, B, DV // 2], F32, name=f"tanh{h}") for h in range(2)]
+        tanh = keep.tile([P, B, DV], F32, name="tanh")
         factor = keep.tile([P, B, DV], F32, name="factor")
 
-        def gate_factor(h):
-            nc.scalar.activation(tanh[h][:], gates[h][:], ACT.Tanh, scale=0.5)
+        def gate_factor():
+            nc.scalar.mul(twice[:], total[:], 2.0)
+            nc.vector.reciprocal(half[:], twice[:])
+            nc.scalar.activation(tanh[:], gate[:], ACT.Tanh, scale=0.5)
             for b in range(B):
-                nc.vector.tensor_scalar(
-                    factor[:, b, h * (DV // 2) : (h + 1) * (DV // 2)], tanh[h][:, b, :], 1.0, half[b][:], ALU.add, ALU.mult
+                nc.scalar.activation(
+                    factor[:, b, :], tanh[:, b, :], ACT.Identity, bias=half[:, b : b + 1], scale=half[:, b : b + 1]
                 )
 
         res = keep.tile([P, B, DV], F32, name="res")
-
-        def attend(e):
-            y = psum.tile([P, B, P], F32, tag="y", bufs=2, name="y")
-            es = slice(e * P, (e + 1) * P)
-            for b in range(B):
-                cols = slice(b * P, (b + 1) * P)
-                nc.tensor.matmul_mx(
-                    out=y[:, b, :],
-                    lhsT=w_codes[b][:].bitcast(FP8X4),
-                    lhsT_scale=w_scales[b][:],
-                    rhs=v_codes[e][:, cols].bitcast(FP8X4),
-                    rhs_scale=v_scales[e][:, cols],
-                    start=True,
-                    stop=True,
-                )
-            nc.vector.tensor_tensor(res[:, :, es], y[:], factor[:, :, es], ALU.mult)
-
         out_rows = out.rearrange("b q e -> q b e")
 
-        def store(first, last):
+        def attend(first, last):
+            width = (last - first) * P
+            y = psum.tile([P, B, width], F32, tag="y", bufs=2, name="y")
+            for b in range(B):
+                cols = slice(b * P, (b + 1) * P)
+                for e in range(first, last):
+                    nc.tensor.matmul_mx(
+                        out=y[:, b, (e - first) * P : (e - first + 1) * P],
+                        lhsT=w_codes[:, cols].bitcast(FP8X4),
+                        lhsT_scale=w_scales[:, cols],
+                        rhs=v_codes[e][:, cols].bitcast(FP8X4),
+                        rhs_scale=v_scales[e][:, cols],
+                        start=True,
+                        stop=True,
+                    )
             es = slice(first * P, last * P)
+            nc.vector.tensor_tensor(res[:, :, es], y[:], factor[:, :, es], ALU.mult)
             nc.sync.dma_start(out_rows[:, :, es], res[:, :, es])
 
         score0 = scores(0)
         score1 = scores(1)
+        gather_values(0, 0, B)
         softmax(0, score0)
-        gather_values(0, False)
         softmax(1, score1)
+        gather_values(1, 0, B)
         weights(0)
-        gather_values(1, False)
         weights(1)
-        quantize_values(0, 0, 2)
-        gather_values(2, False)
-        quantize_values(1, 0, 2)
-        gate_factor(0)
-        attend(0)
-        attend(1)
-        store(0, 2)
-        quantize_values(2, 0, 2)
-        gather_values(3, True)
-        gate_factor(1)
-        attend(2)
-        store(2, 3)
+        quantize_values(0, 0, B)
+        quantize_weights()
+        gate_factor()
+        gather_values(2, 0, B)
+        quantize_values(1, 0, B)
+        gather_values(3, 0, 1)
+        quantize_values(2, 0, B)
+        attend(0, 2)
+        gather_values(3, 1, 2)
+        attend(2, 3)
         quantize_values(3, 0, 1)
         quantize_values(3, 1, 2)
-        attend(3)
-        store(3, 4)
+        attend(3, 4)

@@ -21,7 +21,8 @@ ALU = mybir.AluOpType
 AXIS = mybir.AxisListType
 
 KEY_CHUNK = 1024
-SCALAR_SHARE = [1024, 512, 512, 352]
+SCALAR_SHARE = [1024,384,700,352]
+SCALAR_BLOCKS = [0,1]
 
 
 def tile_attend_gate_kernel(tc, qT, kT, vT, vs, og, offs, out):
@@ -31,24 +32,42 @@ def tile_attend_gate_kernel(tc, qT, kT, vT, vs, og, offs, out):
         psum = ctx.enter_context(tc.psum_pool(name="psum", bufs=1))
 
         lists = keep.tile([P, B * N // 16], U16, name="lists")
-        nc.sync.dma_start(lists[:], offs)
         scale_row = keep.tile([1, T], F32, name="scale_row")
-        nc.sync.dma_start(scale_row[:], vs[0:1, :])
         k_rows = kT.rearrange("(p a h) t -> p a h t", a=2, h=2)
-        k_raw = []
-        for a in range(2):
-            for c in range(T // KEY_CHUNK):
-                raw = keep.tile([P, 2, KEY_CHUNK], F32, name=f"k_raw{a}{c}")
-                nc.sync.dma_start(raw[:], k_rows[:, a, :, c * KEY_CHUNK : (c + 1) * KEY_CHUNK])
-                k_raw.append(raw)
+        k_raw = [
+            keep.tile([P, 2, KEY_CHUNK], F32, tag=f"k_slot{i}", align_bytes=64, name=f"k_raw{i}") for i in range(4)
+        ]
         q_raw = keep.tile([P, B, PACK, NQ], F32, name="q_raw")
-        nc.sync.dma_start(q_raw[:], qT.rearrange("b (p j) q -> p b j q", j=PACK))
-        v_pool = [keep.tile([P, T], F32, name=f"v_pool{e}") for e in range(EB)]
-        gate = keep.tile([P, B, DV], F32, name="gate")
-        for e in range(EB):
-            if e == 2:
-                nc.sync.dma_start(gate[:], og.rearrange("b q e -> q b e"))
+        v_pool = [keep.tile([P, T], F32, tag=f"v_slot{e}", align_bytes=64, name=f"v_pool{e}") for e in range(EB)]
+        gate = [keep.tile([P, B, DV // 2], F32, name=f"gate{h}") for h in range(2)]
+        gate_rows = og.rearrange("b q e -> q b e")
+
+        def load_keys(i):
+            a, c = divmod(i, 2)
+            nc.sync.dma_start(k_raw[i][:], k_rows[:, a, :, c * KEY_CHUNK : (c + 1) * KEY_CHUNK])
+
+        def load_values(e):
             nc.sync.dma_start(v_pool[e][:], vT[e * P : (e + 1) * P, :])
+
+        def load_gate(h):
+            nc.sync.dma_start(gate[h][:], gate_rows[:, :, h * DV // 2 : (h + 1) * DV // 2])
+
+        def load_queries():
+            nc.sync.dma_start(q_raw[:], qT.rearrange("b (p j) q -> p b j q", j=PACK))
+
+        nc.sync.dma_start(lists[:], offs)
+        nc.sync.dma_start(scale_row[:], vs[0:1, :])
+        load_keys(0)
+        load_keys(1)
+        load_keys(2)
+        load_keys(3)
+        load_queries()
+        load_values(0)
+        load_values(1)
+        load_gate(0)
+        load_values(2)
+        load_gate(1)
+        load_values(3)
 
         warm = keep.tile([P, 1], F32, name="warm")
         nc.gpsimd.memset(warm[:], 0.0)
@@ -57,74 +76,115 @@ def tile_attend_gate_kernel(tc, qT, kT, vT, vs, og, offs, out):
         make_identity(nc, ident[:])
 
         scale_pool = keep.tile([P, T], F32, name="scale_pool")
-        nc.vector.memset(scale_pool[:], 0.0)
-        nc.vector.tensor_copy(scale_pool[0:1, :], scale_row[:])
         vs_row = keep.tile([P, B * N], F32, name="vs_row")
-        nc.vector.tensor_copy(vs_row[:], scale_pool[:].indirect(lists[:]))
-        vs_col = []
-        for b in range(B):
-            turned = psum.tile([P, PACK, P], F32, tag="wide", bufs=4, name="turned")
-            for t in range(PACK):
-                nc.tensor.transpose(turned[:, t, :], vs_row[:, b * N + t : (b + 1) * N : PACK], ident[:])
-            col = keep.tile([P, PACK], F32, name=f"vs_col{b}")
-            nc.scalar.copy(col[:], turned[:, :, 0])
-            vs_col.append(col)
+        home = {}
+
+        def token_scales():
+            vs_col = keep.tile([P, B, PACK], F32, tag="k_slot1", align_bytes=64, name="vs_col")
+            home["vs_col"] = vs_col
+            nc.vector.memset(scale_pool[:], 0.0)
+            nc.vector.tensor_copy(scale_pool[0:1, :], scale_row[:])
+            nc.vector.tensor_copy(vs_row[:], scale_pool[:].indirect(lists[:]))
+            for b in range(B):
+                turned = psum.tile([P, PACK, P], F32, tag="wide", bufs=4, name="turned")
+                for t in range(PACK):
+                    nc.tensor.transpose(turned[:, t, :], vs_row[:, b * N + t : (b + 1) * N : PACK], ident[:])
+                nc.scalar.copy(vs_col[:, b, :], turned[:, :, 0])
 
         k_pair = [keep.tile([P, T, 2], BF16, name=f"k_pair{a}") for a in range(2)]
         k_got = keep.tile([P, 2, B * N], U32, name="k_got")
         k_words = keep.tile([P, B * N, 2], U32, align_bytes=64, name="k_words")
         k_codes = keep.tile([P, B * N], U32, align_bytes=64, name="k_codes")
         k_scales = keep.tile([P, B * N], U8, align_bytes=64, name="k_scales")
-        for a in range(2):
-            for c in range(T // KEY_CHUNK):
-                i = a * (T // KEY_CHUNK) + c
-                src = k_raw[i][:].rearrange("p h t -> p t h")
-                first = c * KEY_CHUNK
-                cut = SCALAR_SHARE[i]
-                nc.scalar.activation(k_pair[a][:, first : first + cut, :], src[:, :cut, :], ACT.Copy)
-                if cut < KEY_CHUNK:
-                    nc.vector.tensor_copy(k_pair[a][:, first + cut : first + KEY_CHUNK, :], src[:, cut:, :])
-            window = k_pair[a][:].rearrange("p t h -> p (t h)").bitcast(U32)
-            if a == 0:
-                nc.vector.tensor_copy(k_got[:, a, :], window.indirect(lists[:]))
-            else:
-                for b in range(B):
-                    nc.vector.tensor_copy(
-                        k_got[:, a, b * N : (b + 1) * N], window.indirect(lists[:, b * N // 16 : (b + 1) * N // 16])
-                    )
 
-        q_bf = keep.tile([P, B, NQ, PACK], BF16, align_bytes=64, name="q_bf")
+        def cast_keys(i):
+            a, c = divmod(i, 2)
+            src = k_raw[i][:].rearrange("p h t -> p t h")
+            first = c * KEY_CHUNK
+            cut = SCALAR_SHARE[i]
+            nc.scalar.activation(k_pair[a][:, first : first + cut, :], src[:, :cut, :], ACT.Copy)
+            if cut < KEY_CHUNK:
+                nc.vector.tensor_copy(k_pair[a][:, first + cut : first + KEY_CHUNK, :], src[:, cut:, :])
+
+        def gather_keys(a, first, last):
+            window = k_pair[a][:].rearrange("p t h -> p (t h)").bitcast(U32)
+            nc.vector.tensor_copy(
+                k_got[:, a, first * N : last * N], window.indirect(lists[:, first * N // 16 : last * N // 16])
+            )
+
+        q_and_top = keep.tile([P, B * NQ * 2 + B], F32, tag="q_slot", align_bytes=64, name="q_and_top")
+        q_bf = q_and_top[:, : B * NQ * 2].bitcast(BF16).rearrange("p (b q j) -> p b q j", b=B, j=PACK)
         q_codes = keep.tile([P, B * NQ], U32, align_bytes=64, name="q_codes")
         q_scales = keep.tile([P, B * NQ], U8, align_bytes=64, name="q_scales")
-        nc.scalar.copy(
-            q_bf[:].rearrange("p b (c i) j -> p b c j i", i=4),
-            q_raw[:].rearrange("p b j (c i) -> p b c j i", i=4),
-        )
-        nc.vector.quantize_mx(
-            out=q_codes[:].bitcast(FP8X4), scales=q_scales[:], in_=q_bf[:].rearrange("p b q j -> p (b q j)")
-        )
 
-        minus = [keep.tile([P, 1], F32, name=f"minus{b}") for b in range(B)]
+        def weave_queries(first, last):
+            nc.scalar.copy(
+                q_bf[:, first:last].rearrange("p b (c i) j -> p b c j i", i=4),
+                q_raw[:, first:last].rearrange("p b j (c i) -> p b c j i", i=4),
+            )
+
+        def quantize_queries(first, last):
+            qs = slice(first * NQ, last * NQ)
+            nc.vector.quantize_mx(
+                out=q_codes[:, qs].bitcast(FP8X4),
+                scales=q_scales[:, qs],
+                in_=q_bf[:, first:last].rearrange("p b q j -> p (b q j)"),
+            )
+
+        minus = [q_and_top[:, B * NQ * 2 + b : B * NQ * 2 + b + 1] for b in range(B)]
         total = keep.tile([P, B], F32, name="total")
         twice = keep.tile([P, B], F32, name="twice")
-        half = keep.tile([P, B], F32, name="half")
         weight = [keep.tile([P, PACK, P], F32, name=f"weight{b}") for b in range(B)]
-        w_bf = keep.tile([P, B, NQ, PACK], BF16, align_bytes=64, name="w_bf")
-        w_codes = keep.tile([P, B * NQ], U32, align_bytes=64, name="w_codes")
-        w_scales = keep.tile([P, B * NQ], U8, align_bytes=64, name="w_scales")
+        PART = B * P * 2
+        early = keep.tile([P, 2 * PART], F32, align_bytes=64, name="early")
+        final = keep.tile([P, PART], F32, align_bytes=64, name="final")
+        word_home = {0: early[:, :PART], 1: early[:, PART:], 3: final[:]}
+
+        def place_late():
+            late = keep.tile([P, 2 * PART + B], F32, tag="v_slot2", align_bytes=64, name="late")
+            home["late"] = late
+            home["w_bf"] = late[:, :PART].bitcast(BF16).rearrange("p (b q t) -> p b q t", b=B, t=PACK)
+            home["half"] = late[:, 2 * PART :]
+            word_home[2] = late[:, PART : 2 * PART]
+
+        def place_codes():
+            home["codes"] = keep.tile([P, 5 * B * P], U32, tag="v_slot3", align_bytes=64, name="codes")
+
+        scales = keep.tile([P, 5 * B * P], U8, align_bytes=64, name="scales")
+        v_place = [2, 3, 1, 4]
+
+        def quantize(place, words):
+            cols = slice(place * B * P, place * B * P + words.shape[1] // 2)
+            nc.vector.quantize_mx(
+                out=home["codes"][:, cols].bitcast(FP8X4), scales=scales[:, cols], in_=words.bitcast(BF16)
+            )
+
+        def quantize_x():
+            quantize(0, home["late"][:, : 2 * PART])
+
+        def quantize_y():
+            quantize(2, early[:])
+
+        def quantize_z():
+            quantize(4, final[:])
+
+        score = {}
+
+        def weave_keys(b):
+            s = slice(b * N, (b + 1) * N)
+            nc.scalar.copy(k_words[:, s, :], k_got[:, :, s].rearrange("p a n -> p n a"))
 
         def scores(b):
             s = slice(b * N, (b + 1) * N)
             qs = slice(b * NQ, (b + 1) * NQ)
-            nc.scalar.copy(k_words[:, s, :], k_got[:, :, s].rearrange("p a n -> p n a"))
             nc.vector.quantize_mx(
                 out=k_codes[:, s].bitcast(FP8X4),
                 scales=k_scales[:, s],
                 in_=k_words[:, s, :].rearrange("p n a -> p (n a)").bitcast(BF16),
             )
-            score = psum.tile([P, N], F32, tag="wide", bufs=4, name="score")
+            score[b] = psum.tile([P, N], F32, tag="wide", bufs=4, name="score")
             nc.tensor.matmul_mx(
-                out=score[:],
+                out=score[b][:],
                 lhsT=q_codes[:, qs].bitcast(FP8X4),
                 lhsT_scale=q_scales[:, qs],
                 rhs=k_codes[:, s].bitcast(FP8X4),
@@ -132,72 +192,75 @@ def tile_attend_gate_kernel(tc, qT, kT, vT, vs, og, offs, out):
                 start=True,
                 stop=True,
             )
-            return score
 
-        def softmax(b, score):
-            nc.vector.tensor_reduce(minus[b][:], score[:], axis=AXIS.X, op=ALU.max, negate=True)
+        def softmax(b):
+            nc.vector.tensor_reduce(minus[b], score[b][:], axis=AXIS.X, op=ALU.max, negate=True)
             nc.scalar.activation(
                 weight[b][:],
-                score[:].rearrange("p (c t) -> p t c", t=PACK),
+                score[b][:].rearrange("p (c t) -> p t c", t=PACK),
                 ACT.Exp,
-                bias=minus[b][:],
+                bias=minus[b],
                 accum_out=total[:, b : b + 1],
             )
 
         def weights(b):
-            qs = slice(b * NQ, (b + 1) * NQ)
             turned = psum.tile([P, PACK, P], F32, tag="wide", bufs=4, name="turned")
             for t in range(PACK):
                 nc.tensor.transpose(turned[:, t, :], weight[b][:, t, :], ident[:])
             nc.vector.tensor_tensor(
-                w_bf[:, b, :, :],
+                home["w_bf"][:, b, :, :],
                 turned[:].rearrange("p t q -> p q t"),
-                vs_col[b][:].unsqueeze(1).to_broadcast([P, NQ, PACK]),
+                home["vs_col"][:, b, :].unsqueeze(1).to_broadcast([P, NQ, PACK]),
                 ALU.mult,
             )
 
-        def quantize_weights():
-            nc.vector.quantize_mx(
-                out=w_codes[:].bitcast(FP8X4), scales=w_scales[:], in_=w_bf[:].rearrange("p b q t -> p (b q t)")
-            )
+        v_got = {e: keep.tile([P, 2, B * P, 2], BF16, name=f"v_got{e}") for e in (0, 2, 3)}
 
-        v_got = [keep.tile([P, 2, B * P, 2], BF16, name=f"v_got{e}") for e in range(EB)]
-        v_words = [keep.tile([P, B, P, 2], F32, align_bytes=64, name=f"v_words{e}") for e in range(EB)]
-        v_codes = [keep.tile([P, B * P], U32, align_bytes=64, name=f"v_codes{e}") for e in range(EB)]
-        v_scales = [keep.tile([P, B * P], U8, align_bytes=64, name=f"v_scales{e}") for e in range(EB)]
+        def place_got1():
+            v_got[1] = keep.tile([P, 2, B * P, 2], BF16, tag="q_slot", align_bytes=64, name="v_got1")
+
+        v_cast = {e: keep.tile([P, T], BF16, name=f"v_cast{e}") for e in SCALAR_BLOCKS}
+
+        def cast_values(e):
+            nc.vector.tensor_copy(v_cast[e][:], v_pool[e][:])
 
         def gather_values(e, first, last):
-            nc.vector.tensor_copy(
-                v_got[e][:, :, first * P : last * P, :].rearrange("p u c h -> p c u h"),
-                v_pool[e][:].indirect(lists[:, first * N // 16 : last * N // 16]),
-            )
+            dealt = v_got[e][:, :, first * P : last * P, :].rearrange("p u c h -> p c u h")
+            entries = lists[:, first * N // 16 : last * N // 16]
+            if e in SCALAR_BLOCKS:
+                nc.scalar.activation(dealt, v_cast[e][:].indirect(entries), ACT.Copy)
+            else:
+                nc.vector.tensor_copy(dealt, v_pool[e][:].indirect(entries))
+
+        def turn_values(e, first, last):
             words = v_got[e][:].rearrange("p u c h -> p u (c h)").bitcast(F32)
             turned_v = psum.tile([P, B, 2, P], F32, tag="values", bufs=2, name="turned_v")
             for b in range(first, last):
                 for u in range(2):
                     nc.tensor.transpose(turned_v[:, b, u, :], words[:, u, b * P : (b + 1) * P], ident[:])
+            v_words = word_home[e].rearrange("p (b e u) -> p b e u", b=B, u=2)
             nc.scalar.copy(
-                v_words[e][:, first:last, :, :], turned_v[:, first:last, :, :].rearrange("p b u e -> p b e u")
+                v_words[:, first:last, :, :], turned_v[:, first:last, :, :].rearrange("p b u e -> p b e u")
             )
 
-        def quantize_values(e, first, last):
-            cols = slice(first * P, last * P)
-            nc.vector.quantize_mx(
-                out=v_codes[e][:, cols].bitcast(FP8X4),
-                scales=v_scales[e][:, cols],
-                in_=v_words[e][:, first:last, :, :].rearrange("p b e u -> p (b e u)").bitcast(BF16),
-            )
-
-        tanh = keep.tile([P, B, DV], F32, name="tanh")
+        tanh = [keep.tile([P, B, DV // 2], F32, name=f"tanh{h}") for h in range(2)]
         factor = keep.tile([P, B, DV], F32, name="factor")
 
-        def gate_factor():
-            nc.scalar.mul(twice[:], total[:], 2.0)
-            nc.vector.reciprocal(half[:], twice[:])
-            nc.scalar.activation(tanh[:], gate[:], ACT.Tanh, scale=0.5)
+        def halves():
+            nc.gpsimd.tensor_scalar(twice[:], total[:], 2.0, 0.0, ALU.mult, ALU.add)
+            nc.vector.reciprocal(home["half"], twice[:])
+
+        def gate_tanh(h):
+            nc.scalar.activation(tanh[h][:], gate[h][:], ACT.Tanh, scale=0.5)
+
+        def gate_factor(h):
             for b in range(B):
                 nc.scalar.activation(
-                    factor[:, b, :], tanh[:, b, :], ACT.Identity, bias=half[:, b : b + 1], scale=half[:, b : b + 1]
+                    factor[:, b, h * DV // 2 : (h + 1) * DV // 2],
+                    tanh[h][:, b, :],
+                    ACT.Identity,
+                    bias=home["half"][:, b : b + 1],
+                    scale=home["half"][:, b : b + 1],
                 )
 
         res = keep.tile([P, B, DV], F32, name="res")
@@ -209,12 +272,13 @@ def tile_attend_gate_kernel(tc, qT, kT, vT, vs, og, offs, out):
             for b in range(B):
                 cols = slice(b * P, (b + 1) * P)
                 for e in range(first, last):
+                    at = v_place[e] * B * P + b * P
                     nc.tensor.matmul_mx(
                         out=y[:, b, (e - first) * P : (e - first + 1) * P],
-                        lhsT=w_codes[:, cols].bitcast(FP8X4),
-                        lhsT_scale=w_scales[:, cols],
-                        rhs=v_codes[e][:, cols].bitcast(FP8X4),
-                        rhs_scale=v_scales[e][:, cols],
+                        lhsT=home["codes"][:, cols].bitcast(FP8X4),
+                        lhsT_scale=scales[:, cols],
+                        rhs=home["codes"][:, at : at + P].bitcast(FP8X4),
+                        rhs_scale=scales[:, at : at + P],
                         start=True,
                         stop=True,
                     )
@@ -222,24 +286,49 @@ def tile_attend_gate_kernel(tc, qT, kT, vT, vs, og, offs, out):
             nc.vector.tensor_tensor(res[:, :, es], y[:], factor[:, :, es], ALU.mult)
             nc.sync.dma_start(out_rows[:, :, es], res[:, :, es])
 
-        score0 = scores(0)
-        score1 = scores(1)
-        gather_values(0, 0, B)
-        softmax(0, score0)
-        softmax(1, score1)
-        gather_values(1, 0, B)
+        cast_keys(0)
+        cast_keys(1)
+        token_scales()
+        gather_keys(0, 0, B)
+        cast_keys(2)
+        cast_keys(3)
+        gather_keys(1, 0, 1)
+        gather_keys(1, 1, 2)
+        weave_queries(0, 2)
+        weave_keys(0)
+        weave_keys(1)
+        quantize_queries(0, 2)
+        scores(0)
+        scores(1)
+        cast_values(0)
+        softmax(0)
+        softmax(1)
+        cast_values(1)
+        gather_values(0, 0, 1)
+        gather_values(0, 1, 2)
+        place_got1()
+        gather_values(1, 0, 1)
+        gather_values(1, 1, 2)
+        turn_values(0, 0, B)
+        gather_values(2, 0, B)
+        place_late()
         weights(0)
         weights(1)
-        quantize_values(0, 0, B)
-        quantize_weights()
-        gate_factor()
-        gather_values(2, 0, B)
-        quantize_values(1, 0, B)
+        halves()
+        turn_values(1, 0, B)
+        turn_values(2, 0, B)
         gather_values(3, 0, 1)
-        quantize_values(2, 0, B)
-        attend(0, 2)
         gather_values(3, 1, 2)
+        turn_values(3, 0, 1)
+        gate_tanh(0)
+        gate_tanh(1)
+        turn_values(3, 1, 2)
+        gate_factor(1)
+        gate_factor(0)
+        place_codes()
+        quantize_x()
+        quantize_y()
         attend(2, 3)
-        quantize_values(3, 0, 1)
-        quantize_values(3, 1, 2)
+        quantize_z()
+        attend(0, 2)
         attend(3, 4)

@@ -22,7 +22,7 @@ AXIS = mybir.AxisListType
 
 KEY_CHUNK = 1024
 SCALAR_SHARE = [1024,384,700,352]
-SCALAR_BLOCKS = [0,1]
+SCALAR_BLOCKS = []
 
 
 def tile_attend_gate_kernel(tc, qT, kT, vT, vs, og, offs, out):
@@ -217,7 +217,7 @@ def tile_attend_gate_kernel(tc, qT, kT, vT, vs, og, offs, out):
         v_got = {e: keep.tile([P, 2, B * P, 2], BF16, name=f"v_got{e}") for e in (0, 2, 3)}
 
         def place_got1():
-            v_got[1] = keep.tile([P, 2, B * P, 2], BF16, tag="q_slot", align_bytes=64, name="v_got1")
+            v_got[1] = keep.tile([P, 2, B * P, 2], BF16, name="v_got1")
 
         v_cast = {e: keep.tile([P, T], BF16, name=f"v_cast{e}") for e in SCALAR_BLOCKS}
 
@@ -227,10 +227,7 @@ def tile_attend_gate_kernel(tc, qT, kT, vT, vs, og, offs, out):
         def gather_values(e, first, last):
             dealt = v_got[e][:, :, first * P : last * P, :].rearrange("p u c h -> p c u h")
             entries = lists[:, first * N // 16 : last * N // 16]
-            if e in SCALAR_BLOCKS:
-                nc.scalar.activation(dealt, v_cast[e][:].indirect(entries), ACT.Copy)
-            else:
-                nc.vector.tensor_copy(dealt, v_pool[e][:].indirect(entries))
+            nc.vector.tensor_copy(dealt, v_pool[e][:].indirect(entries))
 
         def turn_values(e, first, last):
             words = v_got[e][:].rearrange("p u c h -> p u (c h)").bitcast(F32)
@@ -300,15 +297,11 @@ def tile_attend_gate_kernel(tc, qT, kT, vT, vs, og, offs, out):
         quantize_queries(0, 2)
         scores(0)
         scores(1)
-        cast_values(0)
+        gather_values(0, 0, B)
         softmax(0)
         softmax(1)
-        cast_values(1)
-        gather_values(0, 0, 1)
-        gather_values(0, 1, 2)
         place_got1()
-        gather_values(1, 0, 1)
-        gather_values(1, 1, 2)
+        gather_values(1, 0, B)
         turn_values(0, 0, B)
         gather_values(2, 0, B)
         place_late()

@@ -9,6 +9,9 @@ FLOPS = 2 * B * NQ * N * (D + DV)
 P = 128
 PACK = 4
 EB = DV // P
+HALF = DV // 2
+CODES = B * P
+WORDS = 2 * CODES
 
 F32 = mybir.dt.float32
 BF16 = mybir.dt.bfloat16
@@ -20,54 +23,47 @@ ACT = mybir.ActivationFunctionType
 ALU = mybir.AluOpType
 AXIS = mybir.AxisListType
 
-KEY_CHUNK = 1024
-SCALAR_SHARE = [1024,384,700,352]
-SCALAR_BLOCKS = []
+KEY_LOADS = [(0, 0, 1024, 1024), (0, 1024, 1024, 384), (1, 0, 1024, 512), (1, 1024, 512, 256), (1, 1536, 512, 176)]
 
 
 def tile_attend_gate_kernel(tc, qT, kT, vT, vs, og, offs, out):
     nc = tc.nc
     with ExitStack() as ctx:
         keep = ctx.enter_context(tc.tile_pool(name="keep", bufs=1))
+        shared = ctx.enter_context(tc.tile_pool(name="shared", bufs=1))
         psum = ctx.enter_context(tc.psum_pool(name="psum", bufs=1))
 
+        ROOM = T * 4
+
+        def room(index, shape, dtype, name, skip=0):
+            return shared.tile(shape, dtype, offset=index * ROOM + skip, align_bytes=64, name=name)
+
+        def entries(first, last):
+            return lists[:, first * N // 16 : last * N // 16]
+
         lists = keep.tile([P, B * N // 16], U16, name="lists")
-        scale_row = keep.tile([1, T], F32, name="scale_row")
-        k_rows = kT.rearrange("(p a h) t -> p a h t", a=2, h=2)
-        k_raw = [
-            keep.tile([P, 2, KEY_CHUNK], F32, tag=f"k_slot{i}", align_bytes=64, name=f"k_raw{i}") for i in range(4)
-        ]
-        q_raw = keep.tile([P, B, PACK, NQ], F32, name="q_raw")
-        v_pool = [keep.tile([P, T], F32, tag=f"v_slot{e}", align_bytes=64, name=f"v_pool{e}") for e in range(EB)]
-        gate = [keep.tile([P, B, DV // 2], F32, name=f"gate{h}") for h in range(2)]
-        gate_rows = og.rearrange("b q e -> q b e")
-
-        def load_keys(i):
-            a, c = divmod(i, 2)
-            nc.sync.dma_start(k_raw[i][:], k_rows[:, a, :, c * KEY_CHUNK : (c + 1) * KEY_CHUNK])
-
-        def load_values(e):
-            nc.sync.dma_start(v_pool[e][:], vT[e * P : (e + 1) * P, :])
-
-        def load_gate(h):
-            nc.sync.dma_start(gate[h][:], gate_rows[:, :, h * DV // 2 : (h + 1) * DV // 2])
-
-        def load_queries():
-            nc.sync.dma_start(q_raw[:], qT.rearrange("b (p j) q -> p b j q", j=PACK))
-
         nc.sync.dma_start(lists[:], offs)
+        scale_row = keep.tile([1, T], F32, name="scale_row")
         nc.sync.dma_start(scale_row[:], vs[0:1, :])
-        load_keys(0)
-        load_keys(1)
-        load_keys(2)
-        load_keys(3)
-        load_queries()
-        load_values(0)
-        load_values(1)
-        load_gate(0)
-        load_values(2)
-        load_gate(1)
-        load_values(3)
+        k_rows = kT.rearrange("(p a h) t -> p a h t", a=2, h=2)
+        k_raw = []
+        for i, (a, first, width, cut) in enumerate(KEY_LOADS):
+            if i == 1:
+                raw = room(EB, [P, 2, width], F32, "k_raw1")
+            else:
+                raw = keep.tile([P, 2, width], F32, name=f"k_raw{i}")
+            nc.sync.dma_start(raw[:], k_rows[:, a, :, first : first + width])
+            k_raw.append(raw)
+        q_raw = keep.tile([P, B, PACK, NQ], F32, name="q_raw")
+        nc.sync.dma_start(q_raw[:], qT.rearrange("b (p j) q -> p b j q", j=PACK))
+        v_pool = [room(e, [P, T], F32, f"v_pool{e}") for e in range(EB)]
+        gate = [keep.tile([P, B, HALF], F32, name=f"gate{h}") for h in range(2)]
+        gate_rows = og.rearrange("b q e -> q b e")
+        for e in range(EB):
+            if e == EB - 1:
+                nc.sync.dma_start(gate[0][:], gate_rows[:, :, :HALF])
+            nc.sync.dma_start(v_pool[e][:], vT[e * P : (e + 1) * P, :])
+        nc.sync.dma_start(gate[1][:], gate_rows[:, :, HALF:])
 
         warm = keep.tile([P, 1], F32, name="warm")
         nc.gpsimd.memset(warm[:], 0.0)
@@ -75,106 +71,59 @@ def tile_attend_gate_kernel(tc, qT, kT, vT, vs, og, offs, out):
         ident = keep.tile([P, P], F32, name="ident")
         make_identity(nc, ident[:])
 
-        scale_pool = keep.tile([P, T], F32, name="scale_pool")
-        vs_row = keep.tile([P, B * N], F32, name="vs_row")
-        home = {}
-
-        def token_scales():
-            vs_col = keep.tile([P, B, PACK], F32, tag="k_slot1", align_bytes=64, name="vs_col")
-            home["vs_col"] = vs_col
-            nc.vector.memset(scale_pool[:], 0.0)
-            nc.vector.tensor_copy(scale_pool[0:1, :], scale_row[:])
-            nc.vector.tensor_copy(vs_row[:], scale_pool[:].indirect(lists[:]))
-            for b in range(B):
-                turned = psum.tile([P, PACK, P], F32, tag="wide", bufs=4, name="turned")
-                for t in range(PACK):
-                    nc.tensor.transpose(turned[:, t, :], vs_row[:, b * N + t : (b + 1) * N : PACK], ident[:])
-                nc.scalar.copy(vs_col[:, b, :], turned[:, :, 0])
-
         k_pair = [keep.tile([P, T, 2], BF16, name=f"k_pair{a}") for a in range(2)]
         k_got = keep.tile([P, 2, B * N], U32, name="k_got")
-        k_words = keep.tile([P, B * N, 2], U32, align_bytes=64, name="k_words")
-        k_codes = keep.tile([P, B * N], U32, align_bytes=64, name="k_codes")
-        k_scales = keep.tile([P, B * N], U8, align_bytes=64, name="k_scales")
 
         def cast_keys(i):
-            a, c = divmod(i, 2)
+            a, first, width, cut = KEY_LOADS[i]
             src = k_raw[i][:].rearrange("p h t -> p t h")
-            first = c * KEY_CHUNK
-            cut = SCALAR_SHARE[i]
             nc.scalar.activation(k_pair[a][:, first : first + cut, :], src[:, :cut, :], ACT.Copy)
-            if cut < KEY_CHUNK:
-                nc.vector.tensor_copy(k_pair[a][:, first + cut : first + KEY_CHUNK, :], src[:, cut:, :])
+            if cut < width:
+                nc.vector.tensor_copy(k_pair[a][:, first + cut : first + width, :], src[:, cut:, :])
 
         def gather_keys(a, first, last):
             window = k_pair[a][:].rearrange("p t h -> p (t h)").bitcast(U32)
-            nc.vector.tensor_copy(
-                k_got[:, a, first * N : last * N], window.indirect(lists[:, first * N // 16 : last * N // 16])
-            )
+            nc.vector.tensor_copy(k_got[:, a, first * N : last * N], window.indirect(entries(first, last)))
 
-        q_and_top = keep.tile([P, B * NQ * 2 + B], F32, tag="q_slot", align_bytes=64, name="q_and_top")
-        q_bf = q_and_top[:, : B * NQ * 2].bitcast(BF16).rearrange("p (b q j) -> p b q j", b=B, j=PACK)
-        q_codes = keep.tile([P, B * NQ], U32, align_bytes=64, name="q_codes")
-        q_scales = keep.tile([P, B * NQ], U8, align_bytes=64, name="q_scales")
+        cast_keys(0)
+        cast_keys(1)
 
-        def weave_queries(first, last):
-            nc.scalar.copy(
-                q_bf[:, first:last].rearrange("p b (c i) j -> p b c j i", i=4),
-                q_raw[:, first:last].rearrange("p b j (c i) -> p b c j i", i=4),
-            )
+        scale_pool = keep.tile([P, T], F32, name="scale_pool")
+        vs_row = keep.tile([P, B * N], F32, name="vs_row")
+        vs_col = room(EB, [P, B, PACK], F32, "vs_col")
+        nc.vector.memset(scale_pool[:], 0.0)
+        nc.vector.tensor_copy(scale_pool[0:1, :], scale_row[:])
+        nc.vector.tensor_copy(vs_row[:], scale_pool[:].indirect(lists[:]))
+        for b in range(B):
+            turned = psum.tile([P, PACK, P], F32, tag="wide", bufs=4, name="turned")
+            for t in range(PACK):
+                nc.tensor.transpose(turned[:, t, :], vs_row[:, b * N + t : (b + 1) * N : PACK], ident[:])
+            nc.scalar.copy(vs_col[:, b, :], turned[:, :, 0])
 
-        def quantize_queries(first, last):
-            qs = slice(first * NQ, last * NQ)
-            nc.vector.quantize_mx(
-                out=q_codes[:, qs].bitcast(FP8X4),
-                scales=q_scales[:, qs],
-                in_=q_bf[:, first:last].rearrange("p b q j -> p (b q j)"),
-            )
-
-        minus = [q_and_top[:, B * NQ * 2 + b : B * NQ * 2 + b + 1] for b in range(B)]
-        total = keep.tile([P, B], F32, name="total")
-        twice = keep.tile([P, B], F32, name="twice")
-        weight = [keep.tile([P, PACK, P], F32, name=f"weight{b}") for b in range(B)]
-        PART = B * P * 2
-        early = keep.tile([P, 2 * PART], F32, align_bytes=64, name="early")
-        final = keep.tile([P, PART], F32, align_bytes=64, name="final")
-        word_home = {0: early[:, :PART], 1: early[:, PART:], 3: final[:]}
-
-        def place_late():
-            late = keep.tile([P, 2 * PART + B], F32, tag="v_slot2", align_bytes=64, name="late")
-            home["late"] = late
-            home["w_bf"] = late[:, :PART].bitcast(BF16).rearrange("p (b q t) -> p b q t", b=B, t=PACK)
-            home["half"] = late[:, 2 * PART :]
-            word_home[2] = late[:, PART : 2 * PART]
-
-        def place_codes():
-            home["codes"] = keep.tile([P, 5 * B * P], U32, tag="v_slot3", align_bytes=64, name="codes")
-
-        scales = keep.tile([P, 5 * B * P], U8, align_bytes=64, name="scales")
-        v_place = [2, 3, 1, 4]
-
-        def quantize(place, words):
-            cols = slice(place * B * P, place * B * P + words.shape[1] // 2)
-            nc.vector.quantize_mx(
-                out=home["codes"][:, cols].bitcast(FP8X4), scales=scales[:, cols], in_=words.bitcast(BF16)
-            )
-
-        def quantize_x():
-            quantize(0, home["late"][:, : 2 * PART])
-
-        def quantize_y():
-            quantize(2, early[:])
-
-        def quantize_z():
-            quantize(4, final[:])
-
-        score = {}
-
-        def weave_keys(b):
+        gather_keys(0, 0, B)
+        for i in range(2, len(KEY_LOADS)):
+            cast_keys(i)
+        k_words = keep.tile([P, B * N, 2], U32, align_bytes=64, name="k_words")
+        for b in range(B):
+            gather_keys(1, b, b + 1)
+        for b in range(B):
             s = slice(b * N, (b + 1) * N)
             nc.scalar.copy(k_words[:, s, :], k_got[:, :, s].rearrange("p a n -> p n a"))
 
-        def scores(b):
+        q_bf = keep.tile([P, B, NQ, PACK], BF16, align_bytes=64, name="q_bf")
+        q_codes = keep.tile([P, B * NQ], U32, align_bytes=64, name="q_codes")
+        q_scales = keep.tile([P, B * NQ], U8, align_bytes=64, name="q_scales")
+        nc.vector.tensor_copy(
+            q_bf[:].rearrange("p b (c i) j -> p b c j i", i=4), q_raw[:].rearrange("p b j (c i) -> p b c j i", i=4)
+        )
+        nc.vector.quantize_mx(
+            out=q_codes[:].bitcast(FP8X4), scales=q_scales[:], in_=q_bf[:].rearrange("p b q j -> p (b q j)")
+        )
+
+        k_codes = keep.tile([P, B * N], U32, align_bytes=64, name="k_codes")
+        k_scales = keep.tile([P, B * N], U8, align_bytes=64, name="k_scales")
+        score = []
+        for b in range(B):
             s = slice(b * N, (b + 1) * N)
             qs = slice(b * NQ, (b + 1) * NQ)
             nc.vector.quantize_mx(
@@ -182,9 +131,9 @@ def tile_attend_gate_kernel(tc, qT, kT, vT, vs, og, offs, out):
                 scales=k_scales[:, s],
                 in_=k_words[:, s, :].rearrange("p n a -> p (n a)").bitcast(BF16),
             )
-            score[b] = psum.tile([P, N], F32, tag="wide", bufs=4, name="score")
+            bank = psum.tile([P, N], F32, tag="wide", bufs=4, name="score")
             nc.tensor.matmul_mx(
-                out=score[b][:],
+                out=bank[:],
                 lhsT=q_codes[:, qs].bitcast(FP8X4),
                 lhsT_scale=q_scales[:, qs],
                 rhs=k_codes[:, s].bitcast(FP8X4),
@@ -192,90 +141,115 @@ def tile_attend_gate_kernel(tc, qT, kT, vT, vs, og, offs, out):
                 start=True,
                 stop=True,
             )
+            score.append(bank)
 
-        def softmax(b):
-            nc.vector.tensor_reduce(minus[b], score[b][:], axis=AXIS.X, op=ALU.max, negate=True)
+        v_cast = keep.tile([P, T], BF16, name="v_cast")
+        nc.scalar.activation(v_cast[:], v_pool[0][:], ACT.Copy)
+
+        minus = keep.tile([P, B], F32, name="minus")
+        total = keep.tile([P, B], F32, name="total")
+        weight = room(0, [P, B, PACK, P], F32, "weight")
+        for b in range(B):
+            nc.vector.tensor_reduce(minus[:, b : b + 1], score[b][:], axis=AXIS.X, op=ALU.max, negate=True)
             nc.scalar.activation(
-                weight[b][:],
+                weight[:, b, :, :],
                 score[b][:].rearrange("p (c t) -> p t c", t=PACK),
                 ACT.Exp,
-                bias=minus[b],
+                bias=minus[:, b : b + 1],
                 accum_out=total[:, b : b + 1],
             )
 
-        def weights(b):
-            turned = psum.tile([P, PACK, P], F32, tag="wide", bufs=4, name="turned")
-            for t in range(PACK):
-                nc.tensor.transpose(turned[:, t, :], weight[b][:, t, :], ident[:])
-            nc.vector.tensor_tensor(
-                home["w_bf"][:, b, :, :],
-                turned[:].rearrange("p t q -> p q t"),
-                home["vs_col"][:, b, :].unsqueeze(1).to_broadcast([P, NQ, PACK]),
-                ALU.mult,
-            )
+        v_got = [keep.tile([P, 2, B * P, 2], BF16, name=f"v_got{e}") for e in range(EB)]
 
-        v_got = {e: keep.tile([P, 2, B * P, 2], BF16, name=f"v_got{e}") for e in (0, 2, 3)}
-
-        def place_got1():
-            v_got[1] = keep.tile([P, 2, B * P, 2], BF16, name="v_got1")
-
-        v_cast = {e: keep.tile([P, T], BF16, name=f"v_cast{e}") for e in SCALAR_BLOCKS}
-
-        def cast_values(e):
-            nc.vector.tensor_copy(v_cast[e][:], v_pool[e][:])
+        def dealt(e, first, last):
+            return v_got[e][:, :, first * P : last * P, :].rearrange("p u c h -> p c u h")
 
         def gather_values(e, first, last):
-            dealt = v_got[e][:, :, first * P : last * P, :].rearrange("p u c h -> p c u h")
-            entries = lists[:, first * N // 16 : last * N // 16]
-            nc.vector.tensor_copy(dealt, v_pool[e][:].indirect(entries))
+            nc.vector.tensor_copy(dealt(e, first, last), v_pool[e][:].indirect(entries(first, last)))
 
-        def turn_values(e, first, last):
+        def turn_values(e, first, last, home):
             words = v_got[e][:].rearrange("p u c h -> p u (c h)").bitcast(F32)
             turned_v = psum.tile([P, B, 2, P], F32, tag="values", bufs=2, name="turned_v")
             for b in range(first, last):
                 for u in range(2):
                     nc.tensor.transpose(turned_v[:, b, u, :], words[:, u, b * P : (b + 1) * P], ident[:])
-            v_words = word_home[e].rearrange("p (b e u) -> p b e u", b=B, u=2)
             nc.scalar.copy(
-                v_words[:, first:last, :, :], turned_v[:, first:last, :, :].rearrange("p b u e -> p b e u")
+                home.rearrange("p (b e u) -> p b e u", b=B, u=2)[:, first:last, :, :],
+                turned_v[:, first:last, :, :].rearrange("p b u e -> p b e u"),
             )
 
-        tanh = [keep.tile([P, B, DV // 2], F32, name=f"tanh{h}") for h in range(2)]
+        gather_values(1, 0, B)
+
+        late = room(1, [P, 2 * WORDS + B], F32, "late")
+        w_bf = late[:, :WORDS].bitcast(BF16).rearrange("p (b q t) -> p b q t", b=B, t=PACK)
+        half = late[:, 2 * WORDS :]
+        for b in range(B):
+            turned = psum.tile([P, PACK, P], F32, tag="wide", bufs=4, name="turned")
+            for t in range(PACK):
+                nc.tensor.transpose(turned[:, t, :], weight[:, b, t, :], ident[:])
+            nc.vector.tensor_tensor(
+                w_bf[:, b, :, :],
+                turned[:].rearrange("p t q -> p q t"),
+                vs_col[:, b, :].unsqueeze(1).to_broadcast([P, NQ, PACK]),
+                ALU.mult,
+            )
+        twice = keep.tile([P, B], F32, name="twice")
+        nc.gpsimd.tensor_scalar(twice[:], total[:], 2.0, 0.0, ALU.mult, ALU.add)
+        nc.vector.reciprocal(half, twice[:])
+
+        nc.scalar.activation(dealt(0, 0, B), v_cast[:].indirect(lists[:]), ACT.Copy)
+        v_words = {e: keep.tile([P, WORDS], F32, align_bytes=64, name=f"v_words{e}") for e in (0, 2, 3)}
+        turn_values(1, 0, B, late[:, WORDS : 2 * WORDS])
+        turn_values(0, 0, B, v_words[0][:])
+        gather_values(2, 0, B)
+        turn_values(2, 0, B, v_words[2][:])
+
+        scales = keep.tile([P, (EB + 1) * CODES], U8, align_bytes=64, name="scales")
+        codes_a = room(2, [P, 3 * CODES], U32, "codes_a")
+
+        def quantize(codes, plane, words):
+            nc.vector.quantize_mx(out=codes.bitcast(FP8X4), scales=plane, in_=words.bitcast(BF16))
+
+        quantize(codes_a[:, : 2 * CODES], scales[:, : 2 * CODES], late[:, : 2 * WORDS])
+        quantize(codes_a[:, 2 * CODES :], scales[:, 2 * CODES : 3 * CODES], v_words[0][:])
+
+        tanh = [keep.tile([P, B, HALF], F32, name=f"tanh{h}") for h in range(2)]
         factor = keep.tile([P, B, DV], F32, name="factor")
 
-        def halves():
-            nc.gpsimd.tensor_scalar(twice[:], total[:], 2.0, 0.0, ALU.mult, ALU.add)
-            nc.vector.reciprocal(home["half"], twice[:])
-
-        def gate_tanh(h):
-            nc.scalar.activation(tanh[h][:], gate[h][:], ACT.Tanh, scale=0.5)
-
         def gate_factor(h):
+            nc.scalar.activation(tanh[h][:], gate[h][:], ACT.Tanh, scale=0.5)
             for b in range(B):
                 nc.scalar.activation(
-                    factor[:, b, h * DV // 2 : (h + 1) * DV // 2],
+                    factor[:, b, h * HALF : (h + 1) * HALF],
                     tanh[h][:, b, :],
                     ACT.Identity,
-                    bias=home["half"][:, b : b + 1],
-                    scale=home["half"][:, b : b + 1],
+                    bias=half[:, b : b + 1],
+                    scale=half[:, b : b + 1],
                 )
 
-        res = keep.tile([P, B, DV], F32, name="res")
+        gate_factor(0)
+        for b in range(B):
+            gather_values(3, b, b + 1)
+        for b in range(B):
+            turn_values(3, b, b + 1, v_words[3][:])
+
+        codes_b = room(3, [P, 2 * CODES], U32, "codes_b")
+        res = room(3, [P, B, DV], F32, "res", skip=2 * CODES * 4)
+        v_codes = [codes_a[:, 2 * CODES :], codes_a[:, CODES : 2 * CODES], codes_b[:, :CODES], codes_b[:, CODES:]]
+        v_plane = [scales[:, place * CODES : (place + 1) * CODES] for place in (2, 1, 3, 4)]
         out_rows = out.rearrange("b q e -> q b e")
 
         def attend(first, last):
-            width = (last - first) * P
-            y = psum.tile([P, B, width], F32, tag="y", bufs=2, name="y")
+            y = psum.tile([P, B, (last - first) * P], F32, tag="y", bufs=2, name="y")
             for b in range(B):
                 cols = slice(b * P, (b + 1) * P)
                 for e in range(first, last):
-                    at = v_place[e] * B * P + b * P
                     nc.tensor.matmul_mx(
                         out=y[:, b, (e - first) * P : (e - first + 1) * P],
-                        lhsT=home["codes"][:, cols].bitcast(FP8X4),
+                        lhsT=codes_a[:, cols].bitcast(FP8X4),
                         lhsT_scale=scales[:, cols],
-                        rhs=home["codes"][:, at : at + P].bitcast(FP8X4),
-                        rhs_scale=scales[:, at : at + P],
+                        rhs=v_codes[e][:, cols].bitcast(FP8X4),
+                        rhs_scale=v_plane[e][:, cols],
                         start=True,
                         stop=True,
                     )
@@ -283,45 +257,9 @@ def tile_attend_gate_kernel(tc, qT, kT, vT, vs, og, offs, out):
             nc.vector.tensor_tensor(res[:, :, es], y[:], factor[:, :, es], ALU.mult)
             nc.sync.dma_start(out_rows[:, :, es], res[:, :, es])
 
-        cast_keys(0)
-        cast_keys(1)
-        token_scales()
-        gather_keys(0, 0, B)
-        cast_keys(2)
-        cast_keys(3)
-        gather_keys(1, 0, 1)
-        gather_keys(1, 1, 2)
-        weave_queries(0, 2)
-        weave_keys(0)
-        weave_keys(1)
-        quantize_queries(0, 2)
-        scores(0)
-        scores(1)
-        gather_values(0, 0, B)
-        softmax(0)
-        softmax(1)
-        place_got1()
-        gather_values(1, 0, B)
-        turn_values(0, 0, B)
-        gather_values(2, 0, B)
-        place_late()
-        weights(0)
-        weights(1)
-        halves()
-        turn_values(1, 0, B)
-        turn_values(2, 0, B)
-        gather_values(3, 0, 1)
-        gather_values(3, 1, 2)
-        turn_values(3, 0, 1)
-        gate_tanh(0)
-        gate_tanh(1)
-        turn_values(3, 1, 2)
-        gate_factor(1)
-        gate_factor(0)
-        place_codes()
-        quantize_x()
-        quantize_y()
-        attend(2, 3)
-        quantize_z()
+        quantize(v_codes[2], v_plane[2], v_words[2][:])
         attend(0, 2)
+        gate_factor(1)
+        quantize(v_codes[3], v_plane[3], v_words[3][:])
+        attend(2, 3)
         attend(3, 4)

@@ -42,22 +42,24 @@ def tile_attend_gate_kernel(tc, qT, kT, vT, vs, og, offs, out):
             return lists[:, first * N // 16 : last * N // 16]
 
         lists = keep.tile([P, B * N // 16], U16, name="lists")
-        nc.sync.dma_start(lists[:], offs)
         scale_row = keep.tile([1, T], F32, name="scale_row")
         nc.sync.dma_start(scale_row[:], vs[0:1, :])
         k_rows = kT.rearrange("(p a h) t -> p a h t", a=2, h=2)
         k_raw = []
         for i, (a, first, width, cut) in enumerate(KEY_LOADS):
             if i == 1:
-                raw = room(EB, [P, 2, width], F32, "k_raw1")
+                raw = room(1, [P, 2, width], F32, "k_raw1")
             else:
                 raw = keep.tile([P, 2, width], F32, name=f"k_raw{i}")
             nc.sync.dma_start(raw[:], k_rows[:, a, :, first : first + width])
             k_raw.append(raw)
+            if i == 0:
+                nc.sync.dma_start(lists[:], offs)
         q_raw = keep.tile([P, B, PACK, NQ], F32, name="q_raw")
         nc.sync.dma_start(q_raw[:], qT.rearrange("b (p j) q -> p b j q", j=PACK))
-        v_pool = [room(e, [P, T], F32, f"v_pool{e}") for e in range(EB)]
-        gate = [keep.tile([P, B, HALF], F32, name=f"gate{h}") for h in range(2)]
+        v_pool = [room(0, [P, T], F32, "v_pool0")]
+        v_pool += [keep.tile([P, T], F32, name=f"v_pool{e}") for e in range(1, EB)]
+        gate = [room(2, [P, B, HALF], F32, "gate0"), keep.tile([P, B, HALF], F32, name="gate1")]
         gate_rows = og.rearrange("b q e -> q b e")
         for e in range(EB):
             if e == EB - 1:
@@ -90,7 +92,7 @@ def tile_attend_gate_kernel(tc, qT, kT, vT, vs, og, offs, out):
 
         scale_pool = keep.tile([P, T], F32, name="scale_pool")
         vs_row = keep.tile([P, B * N], F32, name="vs_row")
-        vs_col = room(EB, [P, B, PACK], F32, "vs_col")
+        vs_col = room(1, [P, B, PACK], F32, "vs_col")
         nc.vector.memset(scale_pool[:], 0.0)
         nc.vector.tensor_copy(scale_pool[0:1, :], scale_row[:])
         nc.vector.tensor_copy(vs_row[:], scale_pool[:].indirect(lists[:]))
@@ -159,20 +161,22 @@ def tile_attend_gate_kernel(tc, qT, kT, vT, vs, og, offs, out):
                 accum_out=total[:, b : b + 1],
             )
 
-        v_got = [keep.tile([P, 2, B * P, 2], BF16, name=f"v_got{e}") for e in range(EB)]
+        v_got = {(e, 0): keep.tile([P, 2, B * P, 2], BF16, name=f"v_got{e}") for e in range(EB - 1)}
+        v_got[(EB - 1, 0)] = room(3, [P, 2, P, 2], BF16, "v_got3a", skip=2 * CODES * 4 - 512)
+        v_got[(EB - 1, 1)] = keep.tile([P, 2, P, 2], BF16, name="v_got3b")
 
-        def dealt(e, first, last):
-            return v_got[e][:, :, first * P : last * P, :].rearrange("p u c h -> p c u h")
+        def dealt(e, first):
+            return v_got[(e, first)][:].rearrange("p u c h -> p c u h")
 
         def gather_values(e, first, last):
-            nc.vector.tensor_copy(dealt(e, first, last), v_pool[e][:].indirect(entries(first, last)))
+            nc.vector.tensor_copy(dealt(e, first), v_pool[e][:].indirect(entries(first, last)))
 
         def turn_values(e, first, last, home):
-            words = v_got[e][:].rearrange("p u c h -> p u (c h)").bitcast(F32)
+            words = v_got[(e, first)][:].rearrange("p u c h -> p u (c h)").bitcast(F32)
             turned_v = psum.tile([P, B, 2, P], F32, tag="values", bufs=2, name="turned_v")
             for b in range(first, last):
                 for u in range(2):
-                    nc.tensor.transpose(turned_v[:, b, u, :], words[:, u, b * P : (b + 1) * P], ident[:])
+                    nc.tensor.transpose(turned_v[:, b, u, :], words[:, u, (b - first) * P : (b - first + 1) * P], ident[:])
             nc.scalar.copy(
                 home.rearrange("p (b e u) -> p b e u", b=B, u=2)[:, first:last, :, :],
                 turned_v[:, first:last, :, :].rearrange("p b u e -> p b e u"),
@@ -180,9 +184,9 @@ def tile_attend_gate_kernel(tc, qT, kT, vT, vs, og, offs, out):
 
         gather_values(1, 0, B)
 
-        late = room(1, [P, 2 * WORDS + B], F32, "late")
+        late = keep.tile([P, 2 * WORDS], F32, align_bytes=64, name="late")
         w_bf = late[:, :WORDS].bitcast(BF16).rearrange("p (b q t) -> p b q t", b=B, t=PACK)
-        half = late[:, 2 * WORDS :]
+        half = keep.tile([P, B], F32, name="half")
         for b in range(B):
             turned = psum.tile([P, PACK, P], F32, tag="wide", bufs=4, name="turned")
             for t in range(PACK):
@@ -195,9 +199,9 @@ def tile_attend_gate_kernel(tc, qT, kT, vT, vs, og, offs, out):
             )
         twice = keep.tile([P, B], F32, name="twice")
         nc.gpsimd.tensor_scalar(twice[:], total[:], 2.0, 0.0, ALU.mult, ALU.add)
-        nc.vector.reciprocal(half, twice[:])
+        nc.vector.reciprocal(half[:], twice[:])
 
-        nc.scalar.activation(dealt(0, 0, B), v_cast[:].indirect(lists[:]), ACT.Copy)
+        nc.scalar.activation(dealt(0, 0), v_cast[:].indirect(lists[:]), ACT.Copy)
         v_words = {e: keep.tile([P, WORDS], F32, align_bytes=64, name=f"v_words{e}") for e in (0, 2, 3)}
         turn_values(1, 0, B, late[:, WORDS : 2 * WORDS])
         turn_values(0, 0, B, v_words[0][:])
@@ -205,19 +209,17 @@ def tile_attend_gate_kernel(tc, qT, kT, vT, vs, og, offs, out):
         turn_values(2, 0, B, v_words[2][:])
 
         scales = keep.tile([P, (EB + 1) * CODES], U8, align_bytes=64, name="scales")
-        codes_a = room(2, [P, 3 * CODES], U32, "codes_a")
 
         def quantize(codes, plane, words):
             nc.vector.quantize_mx(out=codes.bitcast(FP8X4), scales=plane, in_=words.bitcast(BF16))
 
-        quantize(codes_a[:, : 2 * CODES], scales[:, : 2 * CODES], late[:, : 2 * WORDS])
-        quantize(codes_a[:, 2 * CODES :], scales[:, 2 * CODES : 3 * CODES], v_words[0][:])
-
         tanh = [keep.tile([P, B, HALF], F32, name=f"tanh{h}") for h in range(2)]
         factor = keep.tile([P, B, DV], F32, name="factor")
 
-        def gate_factor(h):
+        def gate_tanh(h):
             nc.scalar.activation(tanh[h][:], gate[h][:], ACT.Tanh, scale=0.5)
+
+        def gate_factor(h):
             for b in range(B):
                 nc.scalar.activation(
                     factor[:, b, h * HALF : (h + 1) * HALF],
@@ -227,6 +229,10 @@ def tile_attend_gate_kernel(tc, qT, kT, vT, vs, og, offs, out):
                     scale=half[:, b : b + 1],
                 )
 
+        gate_tanh(0)
+        codes_a = room(2, [P, 3 * CODES], U32, "codes_a")
+        quantize(codes_a[:, : 2 * CODES], scales[:, : 2 * CODES], late[:])
+        quantize(codes_a[:, 2 * CODES :], scales[:, 2 * CODES : 3 * CODES], v_words[0][:])
         gate_factor(0)
         for b in range(B):
             gather_values(3, b, b + 1)
@@ -259,6 +265,7 @@ def tile_attend_gate_kernel(tc, qT, kT, vT, vs, og, offs, out):
 
         quantize(v_codes[2], v_plane[2], v_words[2][:])
         attend(0, 2)
+        gate_tanh(1)
         gate_factor(1)
         quantize(v_codes[3], v_plane[3], v_words[3][:])
         attend(2, 3)

@@ -115,9 +115,7 @@ def tile_attend_gate_kernel(tc, qT, kT, vT, vs, og, offs, out):
         q_bf = keep.tile([P, B, NQ, PACK], BF16, align_bytes=64, name="q_bf")
         q_codes = keep.tile([P, B * NQ], U32, align_bytes=64, name="q_codes")
         q_scales = keep.tile([P, B * NQ], U8, align_bytes=64, name="q_scales")
-        nc.vector.tensor_copy(
-            q_bf[:].rearrange("p b (c i) j -> p b c j i", i=4), q_raw[:].rearrange("p b j (c i) -> p b c j i", i=4)
-        )
+        nc.gpsimd.tensor_scalar(q_bf[:], q_raw[:].rearrange("p b j q -> p b q j"), 1.0, 0.0, ALU.mult, ALU.add)
         nc.vector.quantize_mx(
             out=q_codes[:].bitcast(FP8X4), scales=q_scales[:], in_=q_bf[:].rearrange("p b q j -> p (b q j)")
         )

@@ -23,7 +23,7 @@ ACT = mybir.ActivationFunctionType
 ALU = mybir.AluOpType
 AXIS = mybir.AxisListType
 
-KEY_LOADS = [(0, 0, 1024, 1024), (0, 1024, 1024, 384), (1, 0, 1024, 512), (1, 1024, 512, 256), (1, 1536, 512, 176)]
+KEY_LOADS = [(0, 0, 1024, 1024), (0, 1024, 1024, 384), (1, 0, 1024, 512), (1, 1024, 768, 304), (1, 1792, 256, 88)]
 
 
 def tile_attend_gate_kernel(tc, qT, kT, vT, vs, og, offs, out):
@@ -70,6 +70,8 @@ def tile_attend_gate_kernel(tc, qT, kT, vT, vs, og, offs, out):
         warm = keep.tile([P, 1], F32, name="warm")
         nc.gpsimd.memset(warm[:], 0.0)
         nc.scalar.activation(warm[:], warm[:], ACT.Exp)
+        minus_one = keep.tile([P, B], F32, name="minus_one")
+        nc.gpsimd.memset(minus_one[:], -1.0)
         ident = keep.tile([P, P], F32, name="ident")
         make_identity(nc, ident[:])
 
@@ -197,7 +199,7 @@ def tile_attend_gate_kernel(tc, qT, kT, vT, vs, og, offs, out):
             )
         twice = keep.tile([P, B], F32, name="twice")
         nc.gpsimd.tensor_scalar(twice[:], total[:], 2.0, 0.0, ALU.mult, ALU.add)
-        nc.vector.reciprocal(half[:], twice[:])
+        nc.gpsimd.tensor_tensor(half[:], twice[:], minus_one[:], ALU.pow)
 
         nc.scalar.activation(dealt(0, 0), v_cast[:].indirect(lists[:]), ACT.Copy)
         v_words = {e: keep.tile([P, WORDS], F32, align_bytes=64, name=f"v_words{e}") for e in (0, 2, 3)}

@@ -38,8 +38,8 @@ def tile_attend_gate_kernel(tc, qT, kT, vT, vs, og, offs, out):
         def room(index, shape, dtype, name, skip=0):
             return shared.tile(shape, dtype, offset=index * ROOM + skip, align_bytes=64, name=name)
 
-        def entries(first, last):
-            return lists[:, first * N // 16 : last * N // 16]
+        def entries(first, count):
+            return lists[:, first // 16 : (first + count) // 16]
 
         lists = keep.tile([P, B * N // 16], U16, name="lists")
         scale_row = keep.tile([1, T], F32, name="scale_row")
@@ -47,8 +47,8 @@ def tile_attend_gate_kernel(tc, qT, kT, vT, vs, og, offs, out):
         k_rows = kT.rearrange("(p a h) t -> p a h t", a=2, h=2)
         k_raw = []
         for i, (a, first, width, cut) in enumerate(KEY_LOADS):
-            if i == 1:
-                raw = room(1, [P, 2, width], F32, "k_raw1")
+            if i == len(KEY_LOADS) - 1:
+                raw = room(1, [P, 2, width], F32, "k_raw_last")
             else:
                 raw = keep.tile([P, 2, width], F32, name=f"k_raw{i}")
             nc.sync.dma_start(raw[:], k_rows[:, a, :, first : first + width])
@@ -57,9 +57,9 @@ def tile_attend_gate_kernel(tc, qT, kT, vT, vs, og, offs, out):
                 nc.sync.dma_start(lists[:], offs)
         q_raw = keep.tile([P, B, PACK, NQ], F32, name="q_raw")
         nc.sync.dma_start(q_raw[:], qT.rearrange("b (p j) q -> p b j q", j=PACK))
-        v_pool = [room(0, [P, T], F32, "v_pool0")]
-        v_pool += [keep.tile([P, T], F32, name=f"v_pool{e}") for e in range(1, EB)]
-        gate = [room(2, [P, B, HALF], F32, "gate0"), keep.tile([P, B, HALF], F32, name="gate1")]
+        v_pool = [room(0, [P, T], F32, "v_pool0"), keep.tile([P, T], F32, name="v_pool1")]
+        v_pool += [room(4, [P, T], F32, "v_pool2"), room(5, [P, T], F32, "v_pool3")]
+        gate = [keep.tile([P, B, HALF], F32, name=f"gate{h}") for h in range(2)]
         gate_rows = og.rearrange("b q e -> q b e")
         for e in range(EB):
             if e == EB - 1:
@@ -85,33 +85,37 @@ def tile_attend_gate_kernel(tc, qT, kT, vT, vs, og, offs, out):
             if cut < width:
                 nc.vector.tensor_copy(k_pair[a][:, first + cut : first + width, :], src[:, cut:, :])
 
-        def gather_keys(a, first, last):
+        def gather_keys(a, first, count):
             window = k_pair[a][:].rearrange("p t h -> p (t h)").bitcast(U32)
-            nc.vector.tensor_copy(k_got[:, a, first * N : last * N], window.indirect(entries(first, last)))
+            nc.vector.tensor_copy(k_got[:, a, first : first + count], window.indirect(entries(first, count)))
 
         cast_keys(0)
         cast_keys(1)
 
         scale_pool = keep.tile([P, T], F32, name="scale_pool")
         vs_row = keep.tile([P, B * N], F32, name="vs_row")
-        vs_col = room(1, [P, B, PACK], F32, "vs_col")
         nc.vector.memset(scale_pool[:], 0.0)
         nc.vector.tensor_copy(scale_pool[0:1, :], scale_row[:])
         nc.vector.tensor_copy(vs_row[:], scale_pool[:].indirect(lists[:]))
+        vs_turned = []
         for b in range(B):
-            turned = psum.tile([P, PACK, P], F32, tag="wide", bufs=4, name="turned")
+            turned = psum.tile([P, PACK, P], F32, tag="wide", bufs=5, name="turned")
             for t in range(PACK):
                 nc.tensor.transpose(turned[:, t, :], vs_row[:, b * N + t : (b + 1) * N : PACK], ident[:])
-            nc.scalar.copy(vs_col[:, b, :], turned[:, :, 0])
+            vs_turned.append(turned)
 
-        gather_keys(0, 0, B)
+        gather_keys(0, 0, B * N)
         for i in range(2, len(KEY_LOADS)):
             cast_keys(i)
+        vs_col = room(1, [P, B, PACK], F32, "vs_col")
+        for b in range(B):
+            nc.scalar.copy(vs_col[:, b, :], vs_turned[b][:, :, 0])
         k_words = keep.tile([P, B * N, 2], U32, align_bytes=64, name="k_words")
-        for b in range(B):
-            gather_keys(1, b, b + 1)
-        for b in range(B):
-            s = slice(b * N, (b + 1) * N)
+        pieces = [(0, N // 2), (N // 2, N // 2), (N, N)]
+        for first, count in pieces:
+            gather_keys(1, first, count)
+        for first, count in pieces:
+            s = slice(first, first + count)
             nc.scalar.copy(k_words[:, s, :], k_got[:, :, s].rearrange("p a n -> p n a"))
 
         q_bf = keep.tile([P, B, NQ, PACK], BF16, align_bytes=64, name="q_bf")
@@ -133,7 +137,7 @@ def tile_attend_gate_kernel(tc, qT, kT, vT, vs, og, offs, out):
                 scales=k_scales[:, s],
                 in_=k_words[:, s, :].rearrange("p n a -> p (n a)").bitcast(BF16),
             )
-            bank = psum.tile([P, N], F32, tag="wide", bufs=4, name="score")
+            bank = psum.tile([P, N], F32, tag="wide", bufs=5, name="score")
             nc.tensor.matmul_mx(
                 out=bank[:],
                 lhsT=q_codes[:, qs].bitcast(FP8X4),
@@ -161,22 +165,26 @@ def tile_attend_gate_kernel(tc, qT, kT, vT, vs, og, offs, out):
                 accum_out=total[:, b : b + 1],
             )
 
-        v_got = {(e, 0): keep.tile([P, 2, B * P, 2], BF16, name=f"v_got{e}") for e in range(EB - 1)}
-        v_got[(EB - 1, 0)] = room(3, [P, 2, P, 2], BF16, "v_got3a", skip=2 * CODES * 4 - 512)
-        v_got[(EB - 1, 1)] = keep.tile([P, 2, P, 2], BF16, name="v_got3b")
+        LAST = EB - 1
+        v_got = {(e, 0): keep.tile([P, 2, B * P, 2], BF16, name=f"v_got{e}") for e in range(LAST)}
+        v_got[(LAST, 0)] = keep.tile([P, 2, P, 2], BF16, name="v_got_last0")
+        v_got[(LAST, 1)] = room(3, [P, 2, P, 2], BF16, "v_got_last1")
+        v_words = keep.tile([P, EB * WORDS], F32, align_bytes=64, name="v_words")
+        PLACE = [1, 0, 2, 3]
 
         def dealt(e, first):
             return v_got[(e, first)][:].rearrange("p u c h -> p c u h")
 
         def gather_values(e, first, last):
-            nc.vector.tensor_copy(dealt(e, first), v_pool[e][:].indirect(entries(first, last)))
+            nc.vector.tensor_copy(dealt(e, first), v_pool[e][:].indirect(entries(first * N, (last - first) * N)))
 
-        def turn_values(e, first, last, home):
+        def turn_values(e, first, last):
             words = v_got[(e, first)][:].rearrange("p u c h -> p u (c h)").bitcast(F32)
-            turned_v = psum.tile([P, B, 2, P], F32, tag="values", bufs=2, name="turned_v")
+            turned_v = psum.tile([P, B, 2, P], F32, tag="values", bufs=3, name="turned_v")
             for b in range(first, last):
                 for u in range(2):
                     nc.tensor.transpose(turned_v[:, b, u, :], words[:, u, (b - first) * P : (b - first + 1) * P], ident[:])
+            home = v_words[:, PLACE[e] * WORDS : (PLACE[e] + 1) * WORDS]
             nc.scalar.copy(
                 home.rearrange("p (b e u) -> p b e u", b=B, u=2)[:, first:last, :, :],
                 turned_v[:, first:last, :, :].rearrange("p b u e -> p b e u"),
@@ -184,11 +192,10 @@ def tile_attend_gate_kernel(tc, qT, kT, vT, vs, og, offs, out):
 
         gather_values(1, 0, B)
 
-        late = keep.tile([P, 2 * WORDS], F32, align_bytes=64, name="late")
-        w_bf = late[:, :WORDS].bitcast(BF16).rearrange("p (b q t) -> p b q t", b=B, t=PACK)
+        w_bf = keep.tile([P, B, NQ, PACK], BF16, align_bytes=64, name="w_bf")
         half = keep.tile([P, B], F32, name="half")
         for b in range(B):
-            turned = psum.tile([P, PACK, P], F32, tag="wide", bufs=4, name="turned")
+            turned = psum.tile([P, PACK, P], F32, tag="wide", bufs=5, name="turned")
             for t in range(PACK):
                 nc.tensor.transpose(turned[:, t, :], weight[:, b, t, :], ident[:])
             nc.vector.tensor_tensor(
@@ -202,19 +209,13 @@ def tile_attend_gate_kernel(tc, qT, kT, vT, vs, og, offs, out):
         nc.gpsimd.tensor_tensor(half[:], twice[:], minus_one[:], ALU.pow)
 
         nc.scalar.activation(dealt(0, 0), v_cast[:].indirect(lists[:]), ACT.Copy)
-        v_words = {e: keep.tile([P, WORDS], F32, align_bytes=64, name=f"v_words{e}") for e in (0, 2, 3)}
-        turn_values(1, 0, B, late[:, WORDS : 2 * WORDS])
-        turn_values(0, 0, B, v_words[0][:])
+        turn_values(1, 0, B)
+        turn_values(0, 0, B)
         gather_values(2, 0, B)
-        turn_values(2, 0, B, v_words[2][:])
-
-        scales = keep.tile([P, (EB + 1) * CODES], U8, align_bytes=64, name="scales")
-
-        def quantize(codes, plane, words):
-            nc.vector.quantize_mx(out=codes.bitcast(FP8X4), scales=plane, in_=words.bitcast(BF16))
+        turn_values(2, 0, B)
 
         tanh = [keep.tile([P, B, HALF], F32, name=f"tanh{h}") for h in range(2)]
-        factor = keep.tile([P, B, DV], F32, name="factor")
+        factor = [keep.tile([P, B, HALF], F32, name="factor0"), room(3, [P, B, HALF], F32, "factor1")]
 
         def gate_tanh(h):
             nc.scalar.activation(tanh[h][:], gate[h][:], ACT.Tanh, scale=0.5)
@@ -222,7 +223,7 @@ def tile_attend_gate_kernel(tc, qT, kT, vT, vs, og, offs, out):
         def gate_factor(h):
             for b in range(B):
                 nc.scalar.activation(
-                    factor[:, b, h * HALF : (h + 1) * HALF],
+                    factor[h][:, b, :],
                     tanh[h][:, b, :],
                     ACT.Identity,
                     bias=half[:, b : b + 1],
@@ -230,43 +231,60 @@ def tile_attend_gate_kernel(tc, qT, kT, vT, vs, og, offs, out):
                 )
 
         gate_tanh(0)
-        codes_a = room(2, [P, 3 * CODES], U32, "codes_a")
-        quantize(codes_a[:, : 2 * CODES], scales[:, : 2 * CODES], late[:])
-        quantize(codes_a[:, 2 * CODES :], scales[:, 2 * CODES : 3 * CODES], v_words[0][:])
         gate_factor(0)
         for b in range(B):
-            gather_values(3, b, b + 1)
-        for b in range(B):
-            turn_values(3, b, b + 1, v_words[3][:])
+            gather_values(LAST, b, b + 1)
 
-        codes_b = room(3, [P, 2 * CODES], U32, "codes_b")
-        res = room(3, [P, B, DV], F32, "res", skip=2 * CODES * 4)
-        v_codes = [codes_a[:, 2 * CODES :], codes_a[:, CODES : 2 * CODES], codes_b[:, :CODES], codes_b[:, CODES:]]
-        v_plane = [scales[:, place * CODES : (place + 1) * CODES] for place in (2, 1, 3, 4)]
+        w_codes = room(5, [P, CODES], U32, "w_codes")
+        w_scales = keep.tile([P, CODES], U8, align_bytes=64, name="w_scales")
+        v_codes = room(5, [P, EB * CODES], U32, "v_codes", skip=CODES * 4)
+        v_scales = keep.tile([P, EB * CODES], U8, align_bytes=64, name="v_scales")
+
+        def quantize_values(first, count):
+            nc.vector.quantize_mx(
+                out=v_codes[:, first : first + count].bitcast(FP8X4),
+                scales=v_scales[:, first : first + count],
+                in_=v_words[:, 2 * first : 2 * (first + count)].bitcast(BF16),
+            )
+
+        nc.vector.quantize_mx(
+            out=w_codes[:].bitcast(FP8X4), scales=w_scales[:], in_=w_bf[:].rearrange("p b q t -> p (b q t)")
+        )
+        for place in range(LAST):
+            quantize_values(place * CODES, CODES)
+        gate_tanh(1)
+        for b in range(B):
+            turn_values(LAST, b, b + 1)
+        gate_factor(1)
+        for b in range(B):
+            quantize_values(LAST * CODES + b * P, P)
+
+        res = keep.tile([P, B, DV], F32, name="res")
         out_rows = out.rearrange("b q e -> q b e")
 
-        def attend(first, last):
-            y = psum.tile([P, B, (last - first) * P], F32, tag="y", bufs=2, name="y")
-            for b in range(B):
+        def attend(first, last, seqs):
+            y = psum.tile([P, len(seqs), (last - first) * P], F32, tag="wide", bufs=5, name="y")
+            for i, b in enumerate(seqs):
                 cols = slice(b * P, (b + 1) * P)
                 for e in range(first, last):
+                    v_cols = slice(PLACE[e] * CODES + b * P, PLACE[e] * CODES + (b + 1) * P)
                     nc.tensor.matmul_mx(
-                        out=y[:, b, (e - first) * P : (e - first + 1) * P],
-                        lhsT=codes_a[:, cols].bitcast(FP8X4),
-                        lhsT_scale=scales[:, cols],
-                        rhs=v_codes[e][:, cols].bitcast(FP8X4),
-                        rhs_scale=v_plane[e][:, cols],
+                        out=y[:, i, (e - first) * P : (e - first + 1) * P],
+                        lhsT=w_codes[:, cols].bitcast(FP8X4),
+                        lhsT_scale=w_scales[:, cols],
+                        rhs=v_codes[:, v_cols].bitcast(FP8X4),
+                        rhs_scale=v_scales[:, v_cols],
                         start=True,
                         stop=True,
                     )
             es = slice(first * P, last * P)
-            nc.vector.tensor_tensor(res[:, :, es], y[:], factor[:, :, es], ALU.mult)
-            nc.sync.dma_start(out_rows[:, :, es], res[:, :, es])
+            bs = slice(seqs[0], seqs[-1] + 1)
+            gs = slice(first * P % HALF, (last * P - 1) % HALF + 1)
+            nc.vector.tensor_tensor(res[:, bs, es], y[:], factor[first * P // HALF][:, bs, gs], ALU.mult)
+            nc.sync.dma_start(out_rows[:, bs, es], res[:, bs, es])
 
-        quantize(v_codes[2], v_plane[2], v_words[2][:])
-        attend(0, 2)
-        gate_tanh(1)
-        gate_factor(1)
-        quantize(v_codes[3], v_plane[3], v_words[3][:])
-        attend(2, 3)
-        attend(3, 4)
+        attend(1, 2, [0, 1])
+        attend(0, 1, [0, 1])
+        attend(2, 3, [0, 1])
+        attend(3, 4, [0])
+        attend(3, 4, [1])

@@ -62,9 +62,8 @@ def tile_attend_gate_kernel(tc, qT, kT, vT, vs, og, offs, out):
         gate = [keep.tile([P, B, HALF], F32, name=f"gate{h}") for h in range(2)]
         gate_rows = og.rearrange("b q e -> q b e")
         for e in range(EB):
-            if e == EB - 1:
-                nc.sync.dma_start(gate[0][:], gate_rows[:, :, :HALF])
             nc.sync.dma_start(v_pool[e][:], vT[e * P : (e + 1) * P, :])
+        nc.sync.dma_start(gate[0][:], gate_rows[:, :, :HALF])
         nc.sync.dma_start(gate[1][:], gate_rows[:, :, HALF:])
 
         warm = keep.tile([P, 1], F32, name="warm")
@@ -193,7 +192,7 @@ def tile_attend_gate_kernel(tc, qT, kT, vT, vs, og, offs, out):
         gather_values(1, 0, B)
 
         w_bf = keep.tile([P, B, NQ, PACK], BF16, align_bytes=64, name="w_bf")
-        half = keep.tile([P, B], F32, name="half")
+        inverse = keep.tile([P, B], F32, name="inverse")
         for b in range(B):
             turned = psum.tile([P, PACK, P], F32, tag="wide", bufs=5, name="turned")
             for t in range(PACK):
@@ -204,34 +203,22 @@ def tile_attend_gate_kernel(tc, qT, kT, vT, vs, og, offs, out):
                 vs_col[:, b, :].unsqueeze(1).to_broadcast([P, NQ, PACK]),
                 ALU.mult,
             )
-        twice = keep.tile([P, B], F32, name="twice")
-        nc.gpsimd.tensor_scalar(twice[:], total[:], 2.0, 0.0, ALU.mult, ALU.add)
-        nc.gpsimd.tensor_tensor(half[:], twice[:], minus_one[:], ALU.pow)
+        nc.gpsimd.tensor_tensor(inverse[:], total[:], minus_one[:], ALU.pow)
 
         nc.scalar.activation(dealt(0, 0), v_cast[:].indirect(lists[:]), ACT.Copy)
+        warm_sigmoid = keep.tile([P, 1], F32, name="warm_sigmoid")
+        nc.scalar.activation(warm_sigmoid[:], total[:, 1:2], ACT.Sigmoid)
         turn_values(1, 0, B)
         turn_values(0, 0, B)
         gather_values(2, 0, B)
         turn_values(2, 0, B)
 
-        tanh = [keep.tile([P, B, HALF], F32, name=f"tanh{h}") for h in range(2)]
-        factor = [keep.tile([P, B, HALF], F32, name="factor0"), room(3, [P, B, HALF], F32, "factor1")]
+        sigmoid = [keep.tile([P, B, HALF], F32, name="sigmoid0"), room(3, [P, B, HALF], F32, "sigmoid1")]
 
-        def gate_tanh(h):
-            nc.scalar.activation(tanh[h][:], gate[h][:], ACT.Tanh, scale=0.5)
+        def gate_sigmoid(h):
+            nc.scalar.activation(sigmoid[h][:], gate[h][:], ACT.Sigmoid)
 
-        def gate_factor(h):
-            for b in range(B):
-                nc.scalar.activation(
-                    factor[h][:, b, :],
-                    tanh[h][:, b, :],
-                    ACT.Identity,
-                    bias=half[:, b : b + 1],
-                    scale=half[:, b : b + 1],
-                )
-
-        gate_tanh(0)
-        gate_factor(0)
+        gate_sigmoid(0)
         for b in range(B):
             gather_values(LAST, b, b + 1)
 
@@ -252,39 +239,36 @@ def tile_attend_gate_kernel(tc, qT, kT, vT, vs, og, offs, out):
         )
         for place in range(LAST):
             quantize_values(place * CODES, CODES)
-        gate_tanh(1)
         for b in range(B):
             turn_values(LAST, b, b + 1)
-        gate_factor(1)
+        gate_sigmoid(1)
         for b in range(B):
             quantize_values(LAST * CODES + b * P, P)
 
         res = keep.tile([P, B, DV], F32, name="res")
         out_rows = out.rearrange("b q e -> q b e")
 
-        def attend(first, last, seqs):
-            y = psum.tile([P, len(seqs), (last - first) * P], F32, tag="wide", bufs=5, name="y")
-            for i, b in enumerate(seqs):
-                cols = slice(b * P, (b + 1) * P)
-                for e in range(first, last):
-                    v_cols = slice(PLACE[e] * CODES + b * P, PLACE[e] * CODES + (b + 1) * P)
-                    nc.tensor.matmul_mx(
-                        out=y[:, i, (e - first) * P : (e - first + 1) * P],
-                        lhsT=w_codes[:, cols].bitcast(FP8X4),
-                        lhsT_scale=w_scales[:, cols],
-                        rhs=v_codes[:, v_cols].bitcast(FP8X4),
-                        rhs_scale=v_scales[:, v_cols],
-                        start=True,
-                        stop=True,
-                    )
+        def attend(b, first, last):
+            y = psum.tile([P, (last - first) * P], F32, tag="wide", bufs=5, name="y")
+            cols = slice(b * P, (b + 1) * P)
+            for e in range(first, last):
+                v_first = PLACE[e] * CODES + b * P
+                nc.tensor.matmul_mx(
+                    out=y[:, (e - first) * P : (e - first + 1) * P],
+                    lhsT=w_codes[:, cols].bitcast(FP8X4),
+                    lhsT_scale=w_scales[:, cols],
+                    rhs=v_codes[:, v_first : v_first + P].bitcast(FP8X4),
+                    rhs_scale=v_scales[:, v_first : v_first + P],
+                    start=True,
+                    stop=True,
+                )
             es = slice(first * P, last * P)
-            bs = slice(seqs[0], seqs[-1] + 1)
             gs = slice(first * P % HALF, (last * P - 1) % HALF + 1)
-            nc.vector.tensor_tensor(res[:, bs, es], y[:], factor[first * P // HALF][:, bs, gs], ALU.mult)
-            nc.sync.dma_start(out_rows[:, bs, es], res[:, bs, es])
+            nc.vector.scalar_tensor_tensor(
+                res[:, b, es], y[:], inverse[:, b : b + 1], sigmoid[first * P // HALF][:, b, gs], ALU.mult, ALU.mult
+            )
+            nc.sync.dma_start(out[b, :, es], res[:, b, es])
 
-        attend(1, 2, [0, 1])
-        attend(0, 1, [0, 1])
-        attend(2, 3, [0, 1])
-        attend(3, 4, [0])
-        attend(3, 4, [1])
+        for first, last in [(0, 2), (2, 4)]:
+            for b in range(B):
+                attend(b, first, last)

@@ -167,9 +167,8 @@ def tile_attend_gate_kernel(tc, qT, kT, vT, vs, og, offs, out):
         LAST = EB - 1
         v_got = {(e, 0): keep.tile([P, 2, B * P, 2], BF16, name=f"v_got{e}") for e in range(LAST)}
         v_got[(LAST, 0)] = keep.tile([P, 2, P, 2], BF16, name="v_got_last0")
-        v_got[(LAST, 1)] = room(3, [P, 2, P, 2], BF16, "v_got_last1")
+        v_got[(LAST, 1)] = room(3, [P, 2, P, 2], BF16, "v_got_last1", skip=2048)
         v_words = keep.tile([P, EB * WORDS], F32, align_bytes=64, name="v_words")
-        PLACE = [1, 0, 2, 3]
 
         def dealt(e, first):
             return v_got[(e, first)][:].rearrange("p u c h -> p c u h")
@@ -183,9 +182,9 @@ def tile_attend_gate_kernel(tc, qT, kT, vT, vs, og, offs, out):
             for b in range(first, last):
                 for u in range(2):
                     nc.tensor.transpose(turned_v[:, b, u, :], words[:, u, (b - first) * P : (b - first + 1) * P], ident[:])
-            home = v_words[:, PLACE[e] * WORDS : (PLACE[e] + 1) * WORDS]
+            home = v_words[:].rearrange("p (b f e u) -> p f b e u", b=B, f=EB, u=2)
             nc.scalar.copy(
-                home.rearrange("p (b e u) -> p b e u", b=B, u=2)[:, first:last, :, :],
+                home[:, e, first:last, :, :],
                 turned_v[:, first:last, :, :].rearrange("p b u e -> p b e u"),
             )
 
@@ -198,9 +197,9 @@ def tile_attend_gate_kernel(tc, qT, kT, vT, vs, og, offs, out):
             for t in range(PACK):
                 nc.tensor.transpose(turned[:, t, :], weight[:, b, t, :], ident[:])
             nc.vector.tensor_tensor(
-                w_bf[:, b, :, :],
-                turned[:].rearrange("p t q -> p q t"),
-                vs_col[:, b, :].unsqueeze(1).to_broadcast([P, NQ, PACK]),
+                w_bf[:, b, :, :].rearrange("p (c i) t -> p c t i", i=4),
+                turned[:].rearrange("p t (c i) -> p c t i", i=4),
+                vs_col[:, b, :].unsqueeze(1).unsqueeze(3).to_broadcast([P, NQ // 4, PACK, 4]),
                 ALU.mult,
             )
         nc.gpsimd.tensor_tensor(inverse[:], total[:], minus_one[:], ALU.pow)
@@ -213,12 +212,11 @@ def tile_attend_gate_kernel(tc, qT, kT, vT, vs, og, offs, out):
         gather_values(2, 0, B)
         turn_values(2, 0, B)
 
-        sigmoid = [keep.tile([P, B, HALF], F32, name="sigmoid0"), room(3, [P, B, HALF], F32, "sigmoid1")]
+        sigmoid = [room(3, [P, B, HALF], F32, "sigmoid0", skip=512), room(3, [P, B, HALF], F32, "sigmoid1", skip=2560)]
 
         def gate_sigmoid(h):
             nc.scalar.activation(sigmoid[h][:], gate[h][:], ACT.Sigmoid)
 
-        gate_sigmoid(0)
         for b in range(B):
             gather_values(LAST, b, b + 1)
 
@@ -237,13 +235,14 @@ def tile_attend_gate_kernel(tc, qT, kT, vT, vs, og, offs, out):
         nc.vector.quantize_mx(
             out=w_codes[:].bitcast(FP8X4), scales=w_scales[:], in_=w_bf[:].rearrange("p b q t -> p (b q t)")
         )
-        for place in range(LAST):
-            quantize_values(place * CODES, CODES)
+        for b in range(B):
+            quantize_values(b * DV, HALF)
         for b in range(B):
             turn_values(LAST, b, b + 1)
+        gate_sigmoid(0)
         gate_sigmoid(1)
         for b in range(B):
-            quantize_values(LAST * CODES + b * P, P)
+            quantize_values(b * DV + HALF, HALF)
 
         res = keep.tile([P, B, DV], F32, name="res")
         out_rows = out.rearrange("b q e -> q b e")
@@ -251,17 +250,16 @@ def tile_attend_gate_kernel(tc, qT, kT, vT, vs, og, offs, out):
         def attend(b, first, last):
             y = psum.tile([P, (last - first) * P], F32, tag="wide", bufs=5, name="y")
             cols = slice(b * P, (b + 1) * P)
-            for e in range(first, last):
-                v_first = PLACE[e] * CODES + b * P
-                nc.tensor.matmul_mx(
-                    out=y[:, (e - first) * P : (e - first + 1) * P],
-                    lhsT=w_codes[:, cols].bitcast(FP8X4),
-                    lhsT_scale=w_scales[:, cols],
-                    rhs=v_codes[:, v_first : v_first + P].bitcast(FP8X4),
-                    rhs_scale=v_scales[:, v_first : v_first + P],
-                    start=True,
-                    stop=True,
-                )
+            v_cols = slice(b * DV + first * P, b * DV + last * P)
+            nc.tensor.matmul_mx(
+                out=y[:],
+                lhsT=w_codes[:, cols].bitcast(FP8X4),
+                lhsT_scale=w_scales[:, cols],
+                rhs=v_codes[:, v_cols].bitcast(FP8X4),
+                rhs_scale=v_scales[:, v_cols],
+                start=True,
+                stop=True,
+            )
             es = slice(first * P, last * P)
             gs = slice(first * P % HALF, (last * P - 1) % HALF + 1)
             nc.vector.scalar_tensor_tensor(

@@ -9,9 +9,8 @@ FLOPS = 2 * B * NQ * N * (D + DV)
 P = 128
 PACK = 4
 EB = DV // P
-HALF = DV // 2
-CODES = B * P
-WORDS = 2 * CODES
+LAST = EB - 1
+EARLY = LAST * P
 
 F32 = mybir.dt.float32
 BF16 = mybir.dt.bfloat16
@@ -38,6 +37,9 @@ def tile_attend_gate_kernel(tc, qT, kT, vT, vs, og, offs, out):
         def room(index, shape, dtype, name, skip=0):
             return shared.tile(shape, dtype, offset=index * ROOM + skip, align_bytes=64, name=name)
 
+        def bank(index, shape, name):
+            return psum.tile(shape, F32, tag=f"bank{index}", name=name)
+
         def entries(first, count):
             return lists[:, first // 16 : (first + count) // 16]
 
@@ -57,14 +59,16 @@ def tile_attend_gate_kernel(tc, qT, kT, vT, vs, og, offs, out):
                 nc.sync.dma_start(lists[:], offs)
         q_raw = keep.tile([P, B, PACK, NQ], F32, name="q_raw")
         nc.sync.dma_start(q_raw[:], qT.rearrange("b (p j) q -> p b j q", j=PACK))
-        v_pool = [room(0, [P, T], F32, "v_pool0"), keep.tile([P, T], F32, name="v_pool1")]
-        v_pool += [room(4, [P, T], F32, "v_pool2"), room(5, [P, T], F32, "v_pool3")]
-        gate = [keep.tile([P, B, HALF], F32, name=f"gate{h}") for h in range(2)]
+        v_pool = [keep.tile([P, T], F32, name=f"v_pool{e}") for e in range(LAST)]
+        v_pool.append(room(0, [P, T], F32, "v_pool_last"))
+        gate_early = [keep.tile([P, EARLY], F32, name=f"gate_early{b}") for b in range(B)]
+        gate_late = keep.tile([P, B, P], F32, name="gate_late")
         gate_rows = og.rearrange("b q e -> q b e")
         for e in range(EB):
             nc.sync.dma_start(v_pool[e][:], vT[e * P : (e + 1) * P, :])
-        nc.sync.dma_start(gate[0][:], gate_rows[:, :, :HALF])
-        nc.sync.dma_start(gate[1][:], gate_rows[:, :, HALF:])
+        for b in range(B):
+            nc.sync.dma_start(gate_early[b][:], og[b, :, :EARLY])
+        nc.sync.dma_start(gate_late[:], gate_rows[:, :, EARLY:])
 
         warm = keep.tile([P, 1], F32, name="warm")
         nc.gpsimd.memset(warm[:], 0.0)
@@ -98,7 +102,7 @@ def tile_attend_gate_kernel(tc, qT, kT, vT, vs, og, offs, out):
         nc.vector.tensor_copy(vs_row[:], scale_pool[:].indirect(lists[:]))
         vs_turned = []
         for b in range(B):
-            turned = psum.tile([P, PACK, P], F32, tag="wide", bufs=5, name="turned")
+            turned = bank(b, [P, PACK, P], "vs_turned")
             for t in range(PACK):
                 nc.tensor.transpose(turned[:, t, :], vs_row[:, b * N + t : (b + 1) * N : PACK], ident[:])
             vs_turned.append(turned)
@@ -110,7 +114,7 @@ def tile_attend_gate_kernel(tc, qT, kT, vT, vs, og, offs, out):
         for b in range(B):
             nc.scalar.copy(vs_col[:, b, :], vs_turned[b][:, :, 0])
         k_words = keep.tile([P, B * N, 2], U32, align_bytes=64, name="k_words")
-        pieces = [(0, N // 2), (N // 2, N // 2), (N, N)]
+        pieces = [(first, N // 2) for first in range(0, B * N, N // 2)]
         for first, count in pieces:
             gather_keys(1, first, count)
         for first, count in pieces:
@@ -125,7 +129,7 @@ def tile_attend_gate_kernel(tc, qT, kT, vT, vs, og, offs, out):
             out=q_codes[:].bitcast(FP8X4), scales=q_scales[:], in_=q_bf[:].rearrange("p b q j -> p (b q j)")
         )
 
-        k_codes = keep.tile([P, B * N], U32, align_bytes=64, name="k_codes")
+        k_codes = room(2, [P, B * N], U32, "k_codes")
         k_scales = keep.tile([P, B * N], U8, align_bytes=64, name="k_scales")
         score = []
         for b in range(B):
@@ -136,9 +140,9 @@ def tile_attend_gate_kernel(tc, qT, kT, vT, vs, og, offs, out):
                 scales=k_scales[:, s],
                 in_=k_words[:, s, :].rearrange("p n a -> p (n a)").bitcast(BF16),
             )
-            bank = psum.tile([P, N], F32, tag="wide", bufs=5, name="score")
+            sums = bank(b, [P, N], "score")
             nc.tensor.matmul_mx(
-                out=bank[:],
+                out=sums[:],
                 lhsT=q_codes[:, qs].bitcast(FP8X4),
                 lhsT_scale=q_scales[:, qs],
                 rhs=k_codes[:, s].bitcast(FP8X4),
@@ -146,56 +150,73 @@ def tile_attend_gate_kernel(tc, qT, kT, vT, vs, og, offs, out):
                 start=True,
                 stop=True,
             )
-            score.append(bank)
+            score.append(sums)
 
-        v_cast = keep.tile([P, T], BF16, name="v_cast")
-        nc.scalar.activation(v_cast[:], v_pool[0][:], ACT.Copy)
+        ON_SCALAR = [(0, 1), (2, 0), (2, 1), (3, 1)]
+        HELD = {(0, 0): 2, (1, 0): 3}
+        v_got = {}
+        for e in range(EB):
+            for b in range(B):
+                if (e, b) in HELD:
+                    v_got[(e, b)] = room(HELD[(e, b)], [P, N], BF16, f"v_got{e}{b}", skip=512)
+                else:
+                    v_got[(e, b)] = keep.tile([P, N], BF16, name=f"v_got{e}{b}")
+
+        def gather_values(e, b):
+            picked = v_pool[e][:].indirect(entries(b * N, N))
+            if (e, b) in ON_SCALAR:
+                nc.scalar.activation(v_got[(e, b)][:], picked, ACT.Copy)
+            else:
+                nc.vector.tensor_copy(v_got[(e, b)][:].rearrange("p (u c h) -> p c u h", u=2, h=2), picked)
+
+        def turn(e, b, into):
+            pairs = v_got[(e, b)][:].bitcast(F32)
+            if (e, b) in ON_SCALAR:
+                pairs = pairs.rearrange("p (c u) -> p u c", u=2)
+            else:
+                pairs = pairs.rearrange("p (u c) -> p u c", u=2)
+            for u in range(2):
+                nc.tensor.transpose(into[:, u, :], pairs[:, u, :], ident[:])
+
+        VALUE_BANK = {(1, 0): 0, (1, 1): 7, (2, 0): 4, (2, 1): 5, (3, 0): 6, (3, 1): 0}
+        words = [keep.tile([P, B, P, 2], F32, align_bytes=64, name=f"v_words{e}") for e in range(LAST)]
+        words_last = [keep.tile([P, P, 2], F32, align_bytes=64, name=f"v_words_last{b}") for b in range(B)]
+
+        def turn_block(e):
+            turned_v = bank(1, [P, B, 2, P], "turned_v")
+            for b in range(B):
+                turn(e, b, turned_v[:, b, :, :])
+            nc.scalar.copy(words[e][:], turned_v[:].rearrange("p b u e -> p b e u"))
+
+        def turn_half(e, b):
+            turned_v = bank(VALUE_BANK[(e, b)], [P, 2, P], "turned_half")
+            turn(e, b, turned_v)
+            return turned_v[:].rearrange("p u e -> p e u")
+
+        gather_values(0, 1)
 
         minus = keep.tile([P, B], F32, name="minus")
         total = keep.tile([P, B], F32, name="total")
-        weight = room(0, [P, B, PACK, P], F32, "weight")
+        weight = [keep.tile([P, PACK, P], F32, name=f"weight{b}") for b in range(B)]
         for b in range(B):
             nc.vector.tensor_reduce(minus[:, b : b + 1], score[b][:], axis=AXIS.X, op=ALU.max, negate=True)
             nc.scalar.activation(
-                weight[:, b, :, :],
+                weight[b][:],
                 score[b][:].rearrange("p (c t) -> p t c", t=PACK),
                 ACT.Exp,
                 bias=minus[:, b : b + 1],
                 accum_out=total[:, b : b + 1],
             )
-
-        LAST = EB - 1
-        v_got = {(e, 0): keep.tile([P, 2, B * P, 2], BF16, name=f"v_got{e}") for e in range(LAST)}
-        v_got[(LAST, 0)] = keep.tile([P, 2, P, 2], BF16, name="v_got_last0")
-        v_got[(LAST, 1)] = room(3, [P, 2, P, 2], BF16, "v_got_last1", skip=2048)
-        v_words = keep.tile([P, EB * WORDS], F32, align_bytes=64, name="v_words")
-
-        def dealt(e, first):
-            return v_got[(e, first)][:].rearrange("p u c h -> p c u h")
-
-        def gather_values(e, first, last):
-            nc.vector.tensor_copy(dealt(e, first), v_pool[e][:].indirect(entries(first * N, (last - first) * N)))
-
-        def turn_values(e, first, last):
-            words = v_got[(e, first)][:].rearrange("p u c h -> p u (c h)").bitcast(F32)
-            turned_v = psum.tile([P, B, 2, P], F32, tag="values", bufs=3, name="turned_v")
-            for b in range(first, last):
-                for u in range(2):
-                    nc.tensor.transpose(turned_v[:, b, u, :], words[:, u, (b - first) * P : (b - first + 1) * P], ident[:])
-            home = v_words[:].rearrange("p (b f e u) -> p f b e u", b=B, f=EB, u=2)
-            nc.scalar.copy(
-                home[:, e, first:last, :, :],
-                turned_v[:, first:last, :, :].rearrange("p b u e -> p b e u"),
-            )
-
-        gather_values(1, 0, B)
+        warm_sigmoid = keep.tile([P, 1], F32, name="warm_sigmoid")
+        nc.scalar.activation(warm_sigmoid[:], total[:, 1:2], ACT.Sigmoid)
+        gather_values(0, 0)
 
         w_bf = keep.tile([P, B, NQ, PACK], BF16, align_bytes=64, name="w_bf")
         inverse = keep.tile([P, B], F32, name="inverse")
         for b in range(B):
-            turned = psum.tile([P, PACK, P], F32, tag="wide", bufs=5, name="turned")
+            turned = bank(2 + b, [P, PACK, P], "w_turned")
             for t in range(PACK):
-                nc.tensor.transpose(turned[:, t, :], weight[:, b, t, :], ident[:])
+                nc.tensor.transpose(turned[:, t, :], weight[b][:, t, :], ident[:])
             nc.vector.tensor_tensor(
                 w_bf[:, b, :, :].rearrange("p (c i) t -> p c t i", i=4),
                 turned[:].rearrange("p t (c i) -> p c t i", i=4),
@@ -204,69 +225,74 @@ def tile_attend_gate_kernel(tc, qT, kT, vT, vs, og, offs, out):
             )
         nc.gpsimd.tensor_tensor(inverse[:], total[:], minus_one[:], ALU.pow)
 
-        nc.scalar.activation(dealt(0, 0), v_cast[:].indirect(lists[:]), ACT.Copy)
-        warm_sigmoid = keep.tile([P, 1], F32, name="warm_sigmoid")
-        nc.scalar.activation(warm_sigmoid[:], total[:, 1:2], ACT.Sigmoid)
-        turn_values(1, 0, B)
-        turn_values(0, 0, B)
-        gather_values(2, 0, B)
-        turn_values(2, 0, B)
+        w_scales = keep.tile([P, B * NQ], U8, align_bytes=64, name="w_scales")
+        v_scales = [keep.tile([P, B * P], U8, align_bytes=64, name=f"v_scales{e}") for e in range(LAST)]
+        codes_last = [keep.tile([P, P], U32, align_bytes=64, name=f"codes_last{b}") for b in range(B)]
+        scales_last = [keep.tile([P, P], U8, align_bytes=64, name=f"scales_last{b}") for b in range(B)]
 
-        sigmoid = [room(3, [P, B, HALF], F32, "sigmoid0", skip=512), room(3, [P, B, HALF], F32, "sigmoid1", skip=2560)]
+        def quantize(codes, scales, values):
+            nc.vector.quantize_mx(out=codes.bitcast(FP8X4), scales=scales, in_=values)
 
-        def gate_sigmoid(h):
-            nc.scalar.activation(sigmoid[h][:], gate[h][:], ACT.Sigmoid)
+        def quantize_block(e):
+            quantize(v_codes[e][:], v_scales[e][:], words[e][:].rearrange("p b e u -> p (b e u)").bitcast(BF16))
 
-        for b in range(B):
-            gather_values(LAST, b, b + 1)
-
-        w_codes = room(5, [P, CODES], U32, "w_codes")
-        w_scales = keep.tile([P, CODES], U8, align_bytes=64, name="w_scales")
-        v_codes = room(5, [P, EB * CODES], U32, "v_codes", skip=CODES * 4)
-        v_scales = keep.tile([P, EB * CODES], U8, align_bytes=64, name="v_scales")
-
-        def quantize_values(first, count):
-            nc.vector.quantize_mx(
-                out=v_codes[:, first : first + count].bitcast(FP8X4),
-                scales=v_scales[:, first : first + count],
-                in_=v_words[:, 2 * first : 2 * (first + count)].bitcast(BF16),
-            )
-
-        nc.vector.quantize_mx(
-            out=w_codes[:].bitcast(FP8X4), scales=w_scales[:], in_=w_bf[:].rearrange("p b q t -> p (b q t)")
-        )
-        for b in range(B):
-            quantize_values(b * DV, HALF)
-        for b in range(B):
-            turn_values(LAST, b, b + 1)
-        gate_sigmoid(0)
-        gate_sigmoid(1)
-        for b in range(B):
-            quantize_values(b * DV + HALF, HALF)
-
-        res = keep.tile([P, B, DV], F32, name="res")
-        out_rows = out.rearrange("b q e -> q b e")
-
-        def attend(b, first, last):
-            y = psum.tile([P, (last - first) * P], F32, tag="wide", bufs=5, name="y")
-            cols = slice(b * P, (b + 1) * P)
-            v_cols = slice(b * DV + first * P, b * DV + last * P)
+        def product(y, b, codes, scales):
+            cols = slice(b * NQ, (b + 1) * NQ)
             nc.tensor.matmul_mx(
-                out=y[:],
+                out=y,
                 lhsT=w_codes[:, cols].bitcast(FP8X4),
                 lhsT_scale=w_scales[:, cols],
-                rhs=v_codes[:, v_cols].bitcast(FP8X4),
-                rhs_scale=v_scales[:, v_cols],
+                rhs=codes.bitcast(FP8X4),
+                rhs_scale=scales,
                 start=True,
                 stop=True,
             )
-            es = slice(first * P, last * P)
-            gs = slice(first * P % HALF, (last * P - 1) % HALF + 1)
-            nc.vector.scalar_tensor_tensor(
-                res[:, b, es], y[:], inverse[:, b : b + 1], sigmoid[first * P // HALF][:, b, gs], ALU.mult, ALU.mult
-            )
-            nc.sync.dma_start(out[b, :, es], res[:, b, es])
 
-        for first, last in [(0, 2), (2, 4)]:
+        turn_block(0)
+        for b in range(B):
+            gather_values(1, b)
+        for b in range(B):
+            nc.vector.tensor_copy(words[1][:, b, :, :], turn_half(1, b))
+        for b in range(B):
+            gather_values(2, b)
+        for b in range(B):
+            nc.scalar.copy(words[2][:, b, :, :], turn_half(2, b))
+        w_codes = room(3, [P, B * NQ], U32, "w_codes")
+        v_codes = [room(3, [P, B * P], U32, "v_codes0", skip=1024), keep.tile([P, B * P], U32, align_bytes=64, name="v_codes1")]
+        quantize(w_codes[:], w_scales[:], w_bf[:].rearrange("p b q t -> p (b q t)"))
+        quantize_block(0)
+        quantize_block(1)
+        for b in range(B):
+            gather_values(LAST, b)
+        v_codes.append(room(0, [P, B * P], U32, "v_codes2"))
+        quantize_block(2)
+
+        sigmoid_early = [keep.tile([P, EARLY], F32, name=f"sigmoid_early{b}") for b in range(B)]
+        sigmoid_late = keep.tile([P, B, P], F32, name="sigmoid_late")
+        res_early = [keep.tile([P, EARLY], F32, name=f"res_early{b}") for b in range(B)]
+        res_late = [keep.tile([P, P], F32, name=f"res_late{b}") for b in range(B)]
+
+        def finish(res, y, gate, b, first, last):
+            nc.vector.scalar_tensor_tensor(res, y, inverse[:, b : b + 1], gate, ALU.mult, ALU.mult)
+            nc.sync.dma_start(out[b, :, first:last], res)
+
+        turned_last = [turn_half(LAST, b) for b in range(B)]
+        nc.vector.tensor_copy(words_last[0][:], turned_last[0])
+        nc.scalar.activation(sigmoid_early[0][:], gate_early[0][:], ACT.Sigmoid)
+        nc.scalar.copy(words_last[1][:], turned_last[1])
+        nc.scalar.activation(sigmoid_early[1][:], gate_early[1][:], ACT.Sigmoid)
+        nc.scalar.activation(sigmoid_late[:], gate_late[:], ACT.Sigmoid)
+
+        early = [bank(4 + b, [P, LAST, P], "early") for b in range(B)]
+        for e in range(LAST):
             for b in range(B):
-                attend(b, first, last)
+                cols = slice(b * P, (b + 1) * P)
+                product(early[b][:, e, :], b, v_codes[e][:, cols], v_scales[e][:, cols])
+        late = [bank(2 + b, [P, P], "late") for b in range(B)]
+        finish(res_early[0][:], early[0][:].rearrange("p e c -> p (e c)"), sigmoid_early[0][:], 0, 0, EARLY)
+        for b in range(B):
+            quantize(codes_last[b][:], scales_last[b][:], words_last[b][:].rearrange("p e u -> p (e u)").bitcast(BF16))
+            product(late[b][:], b, codes_last[b][:], scales_last[b][:])
+        finish(res_early[1][:], early[1][:].rearrange("p e c -> p (e c)"), sigmoid_early[1][:], 1, 0, EARLY)
+        for b in range(B):
+            finish(res_late[b][:], late[b][:], sigmoid_late[:, b, :], b, EARLY, DV)

@@ -59,8 +59,7 @@ def tile_attend_gate_kernel(tc, qT, kT, vT, vs, og, offs, out):
                 nc.sync.dma_start(lists[:], offs)
         q_raw = keep.tile([P, B, PACK, NQ], F32, name="q_raw")
         nc.sync.dma_start(q_raw[:], qT.rearrange("b (p j) q -> p b j q", j=PACK))
-        v_pool = [keep.tile([P, T], F32, name=f"v_pool{e}") for e in range(LAST)]
-        v_pool.append(room(0, [P, T], F32, "v_pool_last"))
+        v_pool = [keep.tile([P, T], F32, name=f"v_pool{e}") for e in range(EB)]
         gate_early = [keep.tile([P, EARLY], F32, name=f"gate_early{b}") for b in range(B)]
         gate_late = keep.tile([P, B, P], F32, name="gate_late")
         gate_rows = og.rearrange("b q e -> q b e")
@@ -152,8 +151,8 @@ def tile_attend_gate_kernel(tc, qT, kT, vT, vs, og, offs, out):
             )
             score.append(sums)
 
-        ON_SCALAR = [(0, 1), (2, 0), (2, 1), (3, 1)]
-        HELD = {(0, 0): 2, (1, 0): 3}
+        ON_SCALAR = [(0, 1), (2, 1)]
+        HELD = {(0, 0): 2, (1, 0): 3, (3, 0): 0}
         v_got = {}
         for e in range(EB):
             for b in range(B):
@@ -178,12 +177,12 @@ def tile_attend_gate_kernel(tc, qT, kT, vT, vs, og, offs, out):
             for u in range(2):
                 nc.tensor.transpose(into[:, u, :], pairs[:, u, :], ident[:])
 
-        VALUE_BANK = {(1, 0): 0, (1, 1): 7, (2, 0): 4, (2, 1): 5, (3, 0): 6, (3, 1): 0}
+        VALUE_BANK = {(2, 0): 4, (2, 1): 5, (3, 0): 6, (3, 1): 7}
         words = [keep.tile([P, B, P, 2], F32, align_bytes=64, name=f"v_words{e}") for e in range(LAST)]
         words_last = [keep.tile([P, P, 2], F32, align_bytes=64, name=f"v_words_last{b}") for b in range(B)]
 
         def turn_block(e):
-            turned_v = bank(1, [P, B, 2, P], "turned_v")
+            turned_v = bank(1 - e, [P, B, 2, P], "turned_v")
             for b in range(B):
                 turn(e, b, turned_v[:, b, :, :])
             nc.scalar.copy(words[e][:], turned_v[:].rearrange("p b u e -> p b e u"))
@@ -211,15 +210,20 @@ def tile_attend_gate_kernel(tc, qT, kT, vT, vs, og, offs, out):
         nc.scalar.activation(warm_sigmoid[:], total[:, 1:2], ACT.Sigmoid)
         gather_values(0, 0)
 
-        w_bf = keep.tile([P, B, NQ, PACK], BF16, align_bytes=64, name="w_bf")
         inverse = keep.tile([P, B], F32, name="inverse")
+        w_turned = [bank(2 + b, [P, PACK, P], "w_turned") for b in range(B)]
         for b in range(B):
-            turned = bank(2 + b, [P, PACK, P], "w_turned")
             for t in range(PACK):
-                nc.tensor.transpose(turned[:, t, :], weight[b][:, t, :], ident[:])
+                nc.tensor.transpose(w_turned[b][:, t, :], weight[b][:, t, :], ident[:])
+        turn_block(0)
+        for b in range(B):
+            gather_values(1, b)
+        turn_block(1)
+        w_bf = [room(3, [P, NQ, PACK], BF16, f"w_bf{b}", skip=b * 1024) for b in range(B)]
+        for b in range(B):
             nc.vector.tensor_tensor(
-                w_bf[:, b, :, :].rearrange("p (c i) t -> p c t i", i=4),
-                turned[:].rearrange("p t (c i) -> p c t i", i=4),
+                w_bf[b][:].rearrange("p (c i) t -> p c t i", i=4),
+                w_turned[b][:].rearrange("p t (c i) -> p c t i", i=4),
                 vs_col[:, b, :].unsqueeze(1).unsqueeze(3).to_broadcast([P, NQ // 4, PACK, 4]),
                 ALU.mult,
             )
@@ -248,22 +252,20 @@ def tile_attend_gate_kernel(tc, qT, kT, vT, vs, og, offs, out):
                 stop=True,
             )
 
-        turn_block(0)
+        w_codes = keep.tile([P, B * NQ], U32, align_bytes=64, name="w_codes")
+        v_codes = [keep.tile([P, B * P], U32, align_bytes=64, name=f"v_codes{e}") for e in range(LAST - 1)]
         for b in range(B):
-            gather_values(1, b)
-        for b in range(B):
-            nc.vector.tensor_copy(words[1][:, b, :, :], turn_half(1, b))
+            cols = slice(b * NQ, (b + 1) * NQ)
+            quantize(w_codes[:, cols], w_scales[:, cols], w_bf[b][:].rearrange("p q t -> p (q t)"))
+        quantize_block(0)
+        quantize_block(1)
         for b in range(B):
             gather_values(2, b)
         for b in range(B):
             nc.scalar.copy(words[2][:, b, :, :], turn_half(2, b))
-        w_codes = room(3, [P, B * NQ], U32, "w_codes")
-        v_codes = [room(3, [P, B * P], U32, "v_codes0", skip=1024), keep.tile([P, B * P], U32, align_bytes=64, name="v_codes1")]
-        quantize(w_codes[:], w_scales[:], w_bf[:].rearrange("p b q t -> p (b q t)"))
-        quantize_block(0)
-        quantize_block(1)
         for b in range(B):
             gather_values(LAST, b)
+        turned_last = [turn_half(LAST, b) for b in range(B)]
         v_codes.append(room(0, [P, B * P], U32, "v_codes2"))
         quantize_block(2)
 
@@ -276,11 +278,9 @@ def tile_attend_gate_kernel(tc, qT, kT, vT, vs, og, offs, out):
             nc.vector.scalar_tensor_tensor(res, y, inverse[:, b : b + 1], gate, ALU.mult, ALU.mult)
             nc.sync.dma_start(out[b, :, first:last], res)
 
-        turned_last = [turn_half(LAST, b) for b in range(B)]
-        nc.vector.tensor_copy(words_last[0][:], turned_last[0])
-        nc.scalar.activation(sigmoid_early[0][:], gate_early[0][:], ACT.Sigmoid)
-        nc.scalar.copy(words_last[1][:], turned_last[1])
-        nc.scalar.activation(sigmoid_early[1][:], gate_early[1][:], ACT.Sigmoid)
+        for b in range(B):
+            nc.scalar.activation(sigmoid_early[b][:], gate_early[b][:], ACT.Sigmoid)
+            nc.scalar.copy(words_last[b][:], turned_last[b])
         nc.scalar.activation(sigmoid_late[:], gate_late[:], ACT.Sigmoid)
 
         early = [bank(4 + b, [P, LAST, P], "early") for b in range(B)]

@@ -9,8 +9,9 @@ FLOPS = 2 * B * NQ * N * (D + DV)
 P = 128
 PACK = 4
 EB = DV // P
-LAST = EB - 1
-EARLY = LAST * P
+HALF = DV // 2
+CODES = B * P
+WORDS = 2 * CODES
 
 F32 = mybir.dt.float32
 BF16 = mybir.dt.bfloat16
@@ -59,15 +60,14 @@ def tile_attend_gate_kernel(tc, qT, kT, vT, vs, og, offs, out):
                 nc.sync.dma_start(lists[:], offs)
         q_raw = keep.tile([P, B, PACK, NQ], F32, name="q_raw")
         nc.sync.dma_start(q_raw[:], qT.rearrange("b (p j) q -> p b j q", j=PACK))
-        v_pool = [keep.tile([P, T], F32, name=f"v_pool{e}") for e in range(EB)]
-        gate_early = [keep.tile([P, EARLY], F32, name=f"gate_early{b}") for b in range(B)]
-        gate_late = keep.tile([P, B, P], F32, name="gate_late")
+        v_pool = [keep.tile([P, T], F32, name=f"v_pool{e}") for e in range(EB - 1)]
+        v_pool.append(room(5, [P, T], F32, "v_pool3"))
+        gate = [keep.tile([P, B, HALF], F32, name=f"gate{h}") for h in range(2)]
         gate_rows = og.rearrange("b q e -> q b e")
         for e in range(EB):
             nc.sync.dma_start(v_pool[e][:], vT[e * P : (e + 1) * P, :])
-        for b in range(B):
-            nc.sync.dma_start(gate_early[b][:], og[b, :, :EARLY])
-        nc.sync.dma_start(gate_late[:], gate_rows[:, :, EARLY:])
+        nc.sync.dma_start(gate[0][:], gate_rows[:, :, :HALF])
+        nc.sync.dma_start(gate[1][:], gate_rows[:, :, HALF:])
 
         warm = keep.tile([P, 1], F32, name="warm")
         nc.gpsimd.memset(warm[:], 0.0)
@@ -151,15 +151,18 @@ def tile_attend_gate_kernel(tc, qT, kT, vT, vs, og, offs, out):
             )
             score.append(sums)
 
+        LAST = EB - 1
         ON_SCALAR = [(0, 1), (2, 1)]
-        HELD = {(0, 0): 2, (1, 0): 3, (3, 0): 0}
+        HELD = {(0, 0): (2, 0), (1, 0): (0, 512), (LAST, 1): (3, 2048)}
         v_got = {}
         for e in range(EB):
             for b in range(B):
                 if (e, b) in HELD:
-                    v_got[(e, b)] = room(HELD[(e, b)], [P, N], BF16, f"v_got{e}{b}", skip=512)
+                    v_got[(e, b)] = room(HELD[(e, b)][0], [P, N], BF16, f"v_got{e}{b}", skip=HELD[(e, b)][1])
                 else:
                     v_got[(e, b)] = keep.tile([P, N], BF16, name=f"v_got{e}{b}")
+        v_words = keep.tile([P, EB * WORDS], F32, align_bytes=64, name="v_words")
+        VALUE_BANK = {(0, 0): 1, (1, 0): 0, (2, 0): 4, (LAST, 0): 5, (LAST, 1): 6}
 
         def gather_values(e, b):
             picked = v_pool[e][:].indirect(entries(b * N, N))
@@ -168,29 +171,21 @@ def tile_attend_gate_kernel(tc, qT, kT, vT, vs, og, offs, out):
             else:
                 nc.vector.tensor_copy(v_got[(e, b)][:].rearrange("p (u c h) -> p c u h", u=2, h=2), picked)
 
-        def turn(e, b, into):
-            pairs = v_got[(e, b)][:].bitcast(F32)
-            if (e, b) in ON_SCALAR:
-                pairs = pairs.rearrange("p (c u) -> p u c", u=2)
-            else:
-                pairs = pairs.rearrange("p (u c) -> p u c", u=2)
-            for u in range(2):
-                nc.tensor.transpose(into[:, u, :], pairs[:, u, :], ident[:])
-
-        VALUE_BANK = {(2, 0): 4, (2, 1): 5, (3, 0): 6, (3, 1): 7}
-        words = [keep.tile([P, B, P, 2], F32, align_bytes=64, name=f"v_words{e}") for e in range(LAST)]
-        words_last = [keep.tile([P, P, 2], F32, align_bytes=64, name=f"v_words_last{b}") for b in range(B)]
-
-        def turn_block(e):
-            turned_v = bank(1 - e, [P, B, 2, P], "turned_v")
-            for b in range(B):
-                turn(e, b, turned_v[:, b, :, :])
-            nc.scalar.copy(words[e][:], turned_v[:].rearrange("p b u e -> p b e u"))
-
-        def turn_half(e, b):
-            turned_v = bank(VALUE_BANK[(e, b)], [P, 2, P], "turned_half")
-            turn(e, b, turned_v)
-            return turned_v[:].rearrange("p u e -> p e u")
+        def turn_values(e, first, last):
+            turned_v = bank(VALUE_BANK[(e, first)], [P, B, 2, P], "turned_v")
+            for b in range(first, last):
+                pairs = v_got[(e, b)][:].bitcast(F32)
+                if (e, b) in ON_SCALAR:
+                    pairs = pairs.rearrange("p (c u) -> p u c", u=2)
+                else:
+                    pairs = pairs.rearrange("p (u c) -> p u c", u=2)
+                for u in range(2):
+                    nc.tensor.transpose(turned_v[:, b, u, :], pairs[:, u, :], ident[:])
+            home = v_words[:].rearrange("p (b f e u) -> p f b e u", b=B, f=EB, u=2)
+            nc.scalar.copy(
+                home[:, e, first:last, :, :],
+                turned_v[:, first:last, :, :].rearrange("p b u e -> p b e u"),
+            )
 
         gather_values(0, 1)
 
@@ -215,84 +210,76 @@ def tile_attend_gate_kernel(tc, qT, kT, vT, vs, og, offs, out):
         for b in range(B):
             for t in range(PACK):
                 nc.tensor.transpose(w_turned[b][:, t, :], weight[b][:, t, :], ident[:])
-        turn_block(0)
+        turn_values(0, 0, B)
         for b in range(B):
             gather_values(1, b)
-        turn_block(1)
-        w_bf = [room(3, [P, NQ, PACK], BF16, f"w_bf{b}", skip=b * 1024) for b in range(B)]
+        turn_values(1, 0, B)
+        w_bf = room(0, [P, B, NQ, PACK], BF16, "w_bf")
         for b in range(B):
             nc.vector.tensor_tensor(
-                w_bf[b][:].rearrange("p (c i) t -> p c t i", i=4),
+                w_bf[:, b, :, :].rearrange("p (c i) t -> p c t i", i=4),
                 w_turned[b][:].rearrange("p t (c i) -> p c t i", i=4),
                 vs_col[:, b, :].unsqueeze(1).unsqueeze(3).to_broadcast([P, NQ // 4, PACK, 4]),
                 ALU.mult,
             )
         nc.gpsimd.tensor_tensor(inverse[:], total[:], minus_one[:], ALU.pow)
+        for b in range(B):
+            gather_values(2, b)
+        turn_values(2, 0, B)
+        for b in range(B):
+            gather_values(LAST, b)
 
-        w_scales = keep.tile([P, B * NQ], U8, align_bytes=64, name="w_scales")
-        v_scales = [keep.tile([P, B * P], U8, align_bytes=64, name=f"v_scales{e}") for e in range(LAST)]
-        codes_last = [keep.tile([P, P], U32, align_bytes=64, name=f"codes_last{b}") for b in range(B)]
-        scales_last = [keep.tile([P, P], U8, align_bytes=64, name=f"scales_last{b}") for b in range(B)]
+        sigmoid = [room(3, [P, B, HALF], F32, "sigmoid0", skip=512), room(3, [P, B, HALF], F32, "sigmoid1", skip=2560)]
 
-        def quantize(codes, scales, values):
-            nc.vector.quantize_mx(out=codes.bitcast(FP8X4), scales=scales, in_=values)
+        def gate_sigmoid(h):
+            nc.scalar.activation(sigmoid[h][:], gate[h][:], ACT.Sigmoid)
 
-        def quantize_block(e):
-            quantize(v_codes[e][:], v_scales[e][:], words[e][:].rearrange("p b e u -> p (b e u)").bitcast(BF16))
+        w_codes = room(5, [P, CODES], U32, "w_codes")
+        w_scales = keep.tile([P, CODES], U8, align_bytes=64, name="w_scales")
+        v_codes = room(5, [P, EB * CODES], U32, "v_codes", skip=CODES * 4)
+        v_scales = keep.tile([P, EB * CODES], U8, align_bytes=64, name="v_scales")
 
-        def product(y, b, codes, scales):
-            cols = slice(b * NQ, (b + 1) * NQ)
+        def quantize_values(first, count):
+            nc.vector.quantize_mx(
+                out=v_codes[:, first : first + count].bitcast(FP8X4),
+                scales=v_scales[:, first : first + count],
+                in_=v_words[:, 2 * first : 2 * (first + count)].bitcast(BF16),
+            )
+
+        nc.vector.quantize_mx(
+            out=w_codes[:].bitcast(FP8X4), scales=w_scales[:], in_=w_bf[:].rearrange("p b q t -> p (b q t)")
+        )
+        for b in range(B):
+            quantize_values(b * DV, HALF)
+        for b in range(B):
+            turn_values(LAST, b, b + 1)
+        gate_sigmoid(0)
+        gate_sigmoid(1)
+        for b in range(B):
+            quantize_values(b * DV + HALF, HALF)
+
+        res = keep.tile([P, B, DV], F32, name="res")
+
+        def attend(b, first, last):
+            y = bank(first + b, [P, (last - first) * P], "y")
+            cols = slice(b * P, (b + 1) * P)
+            v_cols = slice(b * DV + first * P, b * DV + last * P)
             nc.tensor.matmul_mx(
-                out=y,
+                out=y[:],
                 lhsT=w_codes[:, cols].bitcast(FP8X4),
                 lhsT_scale=w_scales[:, cols],
-                rhs=codes.bitcast(FP8X4),
-                rhs_scale=scales,
+                rhs=v_codes[:, v_cols].bitcast(FP8X4),
+                rhs_scale=v_scales[:, v_cols],
                 start=True,
                 stop=True,
             )
+            es = slice(first * P, last * P)
+            gs = slice(first * P % HALF, (last * P - 1) % HALF + 1)
+            nc.vector.scalar_tensor_tensor(
+                res[:, b, es], y[:], inverse[:, b : b + 1], sigmoid[first * P // HALF][:, b, gs], ALU.mult, ALU.mult
+            )
+            nc.sync.dma_start(out[b, :, es], res[:, b, es])
 
-        w_codes = keep.tile([P, B * NQ], U32, align_bytes=64, name="w_codes")
-        v_codes = [keep.tile([P, B * P], U32, align_bytes=64, name=f"v_codes{e}") for e in range(LAST - 1)]
-        for b in range(B):
-            cols = slice(b * NQ, (b + 1) * NQ)
-            quantize(w_codes[:, cols], w_scales[:, cols], w_bf[b][:].rearrange("p q t -> p (q t)"))
-        quantize_block(0)
-        quantize_block(1)
-        for b in range(B):
-            gather_values(2, b)
-        for b in range(B):
-            nc.scalar.copy(words[2][:, b, :, :], turn_half(2, b))
-        for b in range(B):
-            gather_values(LAST, b)
-        turned_last = [turn_half(LAST, b) for b in range(B)]
-        v_codes.append(room(0, [P, B * P], U32, "v_codes2"))
-        quantize_block(2)
-
-        sigmoid_early = [keep.tile([P, EARLY], F32, name=f"sigmoid_early{b}") for b in range(B)]
-        sigmoid_late = keep.tile([P, B, P], F32, name="sigmoid_late")
-        res_early = [keep.tile([P, EARLY], F32, name=f"res_early{b}") for b in range(B)]
-        res_late = [keep.tile([P, P], F32, name=f"res_late{b}") for b in range(B)]
-
-        def finish(res, y, gate, b, first, last):
-            nc.vector.scalar_tensor_tensor(res, y, inverse[:, b : b + 1], gate, ALU.mult, ALU.mult)
-            nc.sync.dma_start(out[b, :, first:last], res)
-
-        for b in range(B):
-            nc.scalar.activation(sigmoid_early[b][:], gate_early[b][:], ACT.Sigmoid)
-            nc.scalar.copy(words_last[b][:], turned_last[b])
-        nc.scalar.activation(sigmoid_late[:], gate_late[:], ACT.Sigmoid)
-
-        early = [bank(4 + b, [P, LAST, P], "early") for b in range(B)]
-        for e in range(LAST):
+        for first, last in [(0, 2), (2, 4)]:
             for b in range(B):
-                cols = slice(b * P, (b + 1) * P)
-                product(early[b][:, e, :], b, v_codes[e][:, cols], v_scales[e][:, cols])
-        late = [bank(2 + b, [P, P], "late") for b in range(B)]
-        finish(res_early[0][:], early[0][:].rearrange("p e c -> p (e c)"), sigmoid_early[0][:], 0, 0, EARLY)
-        for b in range(B):
-            quantize(codes_last[b][:], scales_last[b][:], words_last[b][:].rearrange("p e u -> p (e u)").bitcast(BF16))
-            product(late[b][:], b, codes_last[b][:], scales_last[b][:])
-        finish(res_early[1][:], early[1][:].rearrange("p e c -> p (e c)"), sigmoid_early[1][:], 1, 0, EARLY)
-        for b in range(B):
-            finish(res_late[b][:], late[b][:], sigmoid_late[:, b, :], b, EARLY, DV)
+                attend(b, first, last)

@@ -113,7 +113,7 @@ def tile_attend_gate_kernel(tc, qT, kT, vT, vs, og, offs, out):
         for b in range(B):
             nc.scalar.copy(vs_col[:, b, :], vs_turned[b][:, :, 0])
         k_words = keep.tile([P, B * N, 2], U32, align_bytes=64, name="k_words")
-        pieces = [(first, N // 2) for first in range(0, B * N, N // 2)]
+        pieces = [(0, N // 2), (N // 2, N // 2), (N, N)]
         for first, count in pieces:
             gather_keys(1, first, count)
         for first, count in pieces:
@@ -128,7 +128,7 @@ def tile_attend_gate_kernel(tc, qT, kT, vT, vs, og, offs, out):
             out=q_codes[:].bitcast(FP8X4), scales=q_scales[:], in_=q_bf[:].rearrange("p b q j -> p (b q j)")
         )
 
-        k_codes = room(2, [P, B * N], U32, "k_codes")
+        k_codes = keep.tile([P, B * N], U32, align_bytes=64, name="k_codes")
         k_scales = keep.tile([P, B * N], U8, align_bytes=64, name="k_scales")
         score = []
         for b in range(B):
@@ -152,42 +152,48 @@ def tile_attend_gate_kernel(tc, qT, kT, vT, vs, og, offs, out):
             score.append(sums)
 
         LAST = EB - 1
-        ON_SCALAR = [(0, 1), (2, 1)]
-        HELD = {(0, 0): (2, 0), (1, 0): (0, 512), (LAST, 1): (3, 2048)}
+        ON_SCALAR = [(0, 0), (LAST, 1)]
+        SPANS = {(0, 0): 2, (1, 0): 2, (2, 0): 2, (LAST, 0): 1, (LAST, 1): 1}
+        HELD = {(LAST, 1): (3, 2048)}
         v_got = {}
-        for e in range(EB):
-            for b in range(B):
-                if (e, b) in HELD:
-                    v_got[(e, b)] = room(HELD[(e, b)][0], [P, N], BF16, f"v_got{e}{b}", skip=HELD[(e, b)][1])
-                else:
-                    v_got[(e, b)] = keep.tile([P, N], BF16, name=f"v_got{e}{b}")
-        v_words = keep.tile([P, EB * WORDS], F32, align_bytes=64, name="v_words")
+        for (e, b), count in list(SPANS.items()):
+            if (e, b) in HELD:
+                v_got[(e, b)] = room(HELD[(e, b)][0], [P, count * N], BF16, f"v_got{e}{b}", skip=HELD[(e, b)][1])
+            else:
+                v_got[(e, b)] = keep.tile([P, count * N], BF16, name=f"v_got{e}{b}")
+        v_words = [keep.tile([P, B, 2, P, 2], F32, align_bytes=64, name="v_words0")]
         VALUE_BANK = {(0, 0): 1, (1, 0): 0, (2, 0): 4, (LAST, 0): 5, (LAST, 1): 6}
 
         def gather_values(e, b):
-            picked = v_pool[e][:].indirect(entries(b * N, N))
+            picked = v_pool[e][:].indirect(entries(b * N, SPANS[(e, b)] * N))
             if (e, b) in ON_SCALAR:
                 nc.scalar.activation(v_got[(e, b)][:], picked, ACT.Copy)
             else:
                 nc.vector.tensor_copy(v_got[(e, b)][:].rearrange("p (u c h) -> p c u h", u=2, h=2), picked)
 
-        def turn_values(e, first, last):
+        def pairs(e, b):
+            first = b if (e, b) in SPANS else 0
+            words = v_got[(e, first)][:].bitcast(F32)
+            order = "p (c u) -> p u c" if (e, first) in ON_SCALAR else "p (u c) -> p u c"
+            return words.rearrange(order, u=2)[:, :, (b - first) * P : (b - first + 1) * P]
+
+        def turn(e, first, last):
             turned_v = bank(VALUE_BANK[(e, first)], [P, B, 2, P], "turned_v")
             for b in range(first, last):
-                pairs = v_got[(e, b)][:].bitcast(F32)
-                if (e, b) in ON_SCALAR:
-                    pairs = pairs.rearrange("p (c u) -> p u c", u=2)
-                else:
-                    pairs = pairs.rearrange("p (u c) -> p u c", u=2)
                 for u in range(2):
-                    nc.tensor.transpose(turned_v[:, b, u, :], pairs[:, u, :], ident[:])
-            home = v_words[:].rearrange("p (b f e u) -> p f b e u", b=B, f=EB, u=2)
+                    nc.tensor.transpose(turned_v[:, b, u, :], pairs(e, b)[:, u, :], ident[:])
+            return turned_v
+
+        def lay(turned_v, e, first, last):
             nc.scalar.copy(
-                home[:, e, first:last, :, :],
+                v_words[e // 2][:, first:last, e % 2, :, :],
                 turned_v[:, first:last, :, :].rearrange("p b u e -> p b e u"),
             )
 
-        gather_values(0, 1)
+        def turn_values(e, first, last):
+            lay(turn(e, first, last), e, first, last)
+
+        gather_values(0, 0)
 
         minus = keep.tile([P, B], F32, name="minus")
         total = keep.tile([P, B], F32, name="total")
@@ -203,7 +209,7 @@ def tile_attend_gate_kernel(tc, qT, kT, vT, vs, og, offs, out):
             )
         warm_sigmoid = keep.tile([P, 1], F32, name="warm_sigmoid")
         nc.scalar.activation(warm_sigmoid[:], total[:, 1:2], ACT.Sigmoid)
-        gather_values(0, 0)
+        gather_values(1, 0)
 
         inverse = keep.tile([P, B], F32, name="inverse")
         w_turned = [bank(2 + b, [P, PACK, P], "w_turned") for b in range(B)]
@@ -211,10 +217,7 @@ def tile_attend_gate_kernel(tc, qT, kT, vT, vs, og, offs, out):
             for t in range(PACK):
                 nc.tensor.transpose(w_turned[b][:, t, :], weight[b][:, t, :], ident[:])
         turn_values(0, 0, B)
-        for b in range(B):
-            gather_values(1, b)
-        turn_values(1, 0, B)
-        w_bf = room(0, [P, B, NQ, PACK], BF16, "w_bf")
+        w_bf = keep.tile([P, B, NQ, PACK], BF16, align_bytes=64, name="w_bf")
         for b in range(B):
             nc.vector.tensor_tensor(
                 w_bf[:, b, :, :].rearrange("p (c i) t -> p c t i", i=4),
@@ -223,11 +226,14 @@ def tile_attend_gate_kernel(tc, qT, kT, vT, vs, og, offs, out):
                 ALU.mult,
             )
         nc.gpsimd.tensor_tensor(inverse[:], total[:], minus_one[:], ALU.pow)
-        for b in range(B):
-            gather_values(2, b)
-        turn_values(2, 0, B)
+        turn_values(1, 0, B)
+        gather_values(2, 0)
+        turned_two = turn(2, 0, B)
         for b in range(B):
             gather_values(LAST, b)
+        turned_last = [turn(LAST, b, b + 1) for b in range(B)]
+        v_words.append(room(5, [P, B, 2, P, 2], F32, "v_words1", skip=(EB + 1) * CODES * 4))
+        lay(turned_two, 2, 0, B)
 
         sigmoid = [room(3, [P, B, HALF], F32, "sigmoid0", skip=512), room(3, [P, B, HALF], F32, "sigmoid1", skip=2560)]
 
@@ -239,24 +245,25 @@ def tile_attend_gate_kernel(tc, qT, kT, vT, vs, og, offs, out):
         v_codes = room(5, [P, EB * CODES], U32, "v_codes", skip=CODES * 4)
         v_scales = keep.tile([P, EB * CODES], U8, align_bytes=64, name="v_scales")
 
-        def quantize_values(first, count):
+        def quantize_values(b, h):
+            cols = slice(b * DV + h * HALF, b * DV + (h + 1) * HALF)
             nc.vector.quantize_mx(
-                out=v_codes[:, first : first + count].bitcast(FP8X4),
-                scales=v_scales[:, first : first + count],
-                in_=v_words[:, 2 * first : 2 * (first + count)].bitcast(BF16),
+                out=v_codes[:, cols].bitcast(FP8X4),
+                scales=v_scales[:, cols],
+                in_=v_words[h][:, b, :, :, :].rearrange("p f e u -> p (f e u)").bitcast(BF16),
             )
 
         nc.vector.quantize_mx(
             out=w_codes[:].bitcast(FP8X4), scales=w_scales[:], in_=w_bf[:].rearrange("p b q t -> p (b q t)")
         )
         for b in range(B):
-            quantize_values(b * DV, HALF)
+            quantize_values(b, 0)
         for b in range(B):
-            turn_values(LAST, b, b + 1)
+            lay(turned_last[b], LAST, b, b + 1)
         gate_sigmoid(0)
         gate_sigmoid(1)
         for b in range(B):
-            quantize_values(b * DV + HALF, HALF)
+            quantize_values(b, 1)
 
         res = keep.tile([P, B, DV], F32, name="res")
 

@@ -113,7 +113,7 @@ def tile_attend_gate_kernel(tc, qT, kT, vT, vs, og, offs, out):
         for b in range(B):
             nc.scalar.copy(vs_col[:, b, :], vs_turned[b][:, :, 0])
         k_words = keep.tile([P, B * N, 2], U32, align_bytes=64, name="k_words")
-        pieces = [(0, N // 2), (N // 2, N // 2), (N, N)]
+        pieces = [(first, N // 2) for first in range(0, B * N, N // 2)]
         for first, count in pieces:
             gather_keys(1, first, count)
         for first, count in pieces:
@@ -184,8 +184,8 @@ def tile_attend_gate_kernel(tc, qT, kT, vT, vs, og, offs, out):
                     nc.tensor.transpose(turned_v[:, b, u, :], pairs(e, b)[:, u, :], ident[:])
             return turned_v
 
-        def lay(turned_v, e, first, last):
-            nc.scalar.copy(
+        def lay(turned_v, e, first, last, copy=nc.scalar.copy):
+            copy(
                 v_words[e // 2][:, first:last, e % 2, :, :],
                 turned_v[:, first:last, :, :].rearrange("p b u e -> p b e u"),
             )
@@ -256,10 +256,10 @@ def tile_attend_gate_kernel(tc, qT, kT, vT, vs, og, offs, out):
         nc.vector.quantize_mx(
             out=w_codes[:].bitcast(FP8X4), scales=w_scales[:], in_=w_bf[:].rearrange("p b q t -> p (b q t)")
         )
-        for b in range(B):
-            quantize_values(b, 0)
-        for b in range(B):
-            lay(turned_last[b], LAST, b, b + 1)
+        quantize_values(0, 0)
+        lay(turned_last[0], LAST, 0, 1, nc.vector.tensor_copy)
+        quantize_values(1, 0)
+        lay(turned_last[1], LAST, 1, 2)
         gate_sigmoid(0)
         gate_sigmoid(1)
         for b in range(B):

@@ -11,6 +11,7 @@ PACK = 4
 EB = DV // P
 HALF = DV // 2
 CODES = B * P
+ROW = 256
 WORDS = 2 * CODES
 
 F32 = mybir.dt.float32
@@ -36,7 +37,7 @@ def tile_attend_gate_kernel(tc, qT, kT, vT, vs, og, offs, out):
         ROOM = T * 4
 
         def room(index, shape, dtype, name, skip=0):
-            return shared.tile(shape, dtype, offset=index * ROOM + skip, align_bytes=64, name=name)
+            return shared.tile(shape, dtype, offset=index * ROOM + skip, align_bytes=ROW, name=name)
 
         def bank(index, shape, name):
             return psum.tile(shape, F32, tag=f"bank{index}", name=name)
@@ -45,7 +46,7 @@ def tile_attend_gate_kernel(tc, qT, kT, vT, vs, og, offs, out):
             return lists[:, first // 16 : (first + count) // 16]
 
         lists = keep.tile([P, B * N // 16], U16, name="lists")
-        scale_row = keep.tile([1, T], F32, name="scale_row")
+        scale_row = keep.tile([1, T], F32, align_bytes=ROW, name="scale_row")
         nc.sync.dma_start(scale_row[:], vs[0:1, :])
         k_rows = kT.rearrange("(p a h) t -> p a h t", a=2, h=2)
         k_raw = []
@@ -53,27 +54,26 @@ def tile_attend_gate_kernel(tc, qT, kT, vT, vs, og, offs, out):
             if i == len(KEY_LOADS) - 1:
                 raw = room(1, [P, 2, width], F32, "k_raw_last")
             else:
-                raw = keep.tile([P, 2, width], F32, name=f"k_raw{i}")
+                raw = keep.tile([P, 2, width], F32, align_bytes=ROW, name=f"k_raw{i}")
             nc.sync.dma_start(raw[:], k_rows[:, a, :, first : first + width])
             k_raw.append(raw)
             if i == 0:
                 nc.sync.dma_start(lists[:], offs)
-        q_raw = keep.tile([P, B, PACK, NQ], F32, name="q_raw")
+        q_raw = keep.tile([P, B, PACK, NQ], F32, align_bytes=ROW, name="q_raw")
         nc.sync.dma_start(q_raw[:], qT.rearrange("b (p j) q -> p b j q", j=PACK))
-        v_pool = [keep.tile([P, T], F32, name=f"v_pool{e}") for e in range(EB - 1)]
+        v_pool = [keep.tile([P, T], F32, align_bytes=ROW, name=f"v_pool{e}") for e in range(EB - 1)]
         v_pool.append(room(5, [P, T], F32, "v_pool3"))
-        gate = [keep.tile([P, B, HALF], F32, name=f"gate{h}") for h in range(2)]
+        gate = [keep.tile([P, B, HALF], F32, align_bytes=ROW, name=f"gate{h}") for h in range(2)]
         gate_rows = og.rearrange("b q e -> q b e")
         for e in range(EB):
             nc.sync.dma_start(v_pool[e][:], vT[e * P : (e + 1) * P, :])
         nc.sync.dma_start(gate[0][:], gate_rows[:, :, :HALF])
         nc.sync.dma_start(gate[1][:], gate_rows[:, :, HALF:])
 
-        warm = keep.tile([P, 1], F32, name="warm")
-        nc.gpsimd.memset(warm[:], 0.0)
-        nc.scalar.activation(warm[:], warm[:], ACT.Exp)
         minus_one = keep.tile([P, B], F32, name="minus_one")
         nc.gpsimd.memset(minus_one[:], -1.0)
+        warm = keep.tile([P, 1], F32, name="warm")
+        nc.scalar.activation(warm[:], minus_one[:, 0:1], ACT.Exp)
         ident = keep.tile([P, P], F32, name="ident")
         make_identity(nc, ident[:])
 
@@ -195,7 +195,7 @@ def tile_attend_gate_kernel(tc, qT, kT, vT, vs, og, offs, out):
 
         gather_values(0, 0)
 
-        minus = keep.tile([P, B], F32, name="minus")
+        minus = room(2, [P, B], F32, "minus")
         total = keep.tile([P, B], F32, name="total")
         weight = [keep.tile([P, PACK, P], F32, name=f"weight{b}") for b in range(B)]
         for b in range(B):
@@ -207,8 +207,8 @@ def tile_attend_gate_kernel(tc, qT, kT, vT, vs, og, offs, out):
                 bias=minus[:, b : b + 1],
                 accum_out=total[:, b : b + 1],
             )
-        warm_sigmoid = keep.tile([P, 1], F32, name="warm_sigmoid")
-        nc.scalar.activation(warm_sigmoid[:], total[:, 1:2], ACT.Sigmoid)
+        warm_sigmoid = room(2, [P, 1], F32, "warm_sigmoid")
+        nc.scalar.activation(warm_sigmoid[:], minus_one[:, 0:1], ACT.Sigmoid)
         gather_values(1, 0)
 
         inverse = keep.tile([P, B], F32, name="inverse")
@@ -265,7 +265,7 @@ def tile_attend_gate_kernel(tc, qT, kT, vT, vs, og, offs, out):
         for b in range(B):
             quantize_values(b, 1)
 
-        res = keep.tile([P, B, DV], F32, name="res")
+        res = keep.tile([P, B, DV], F32, align_bytes=ROW, name="res")
 
         def attend(b, first, last):
             y = bank(first + b, [P, (last - first) * P], "y")

@@ -167,15 +167,14 @@ def tile_attend_gate_kernel(tc, qT, kT, vT, vs, og, offs, out):
         def gather_values(e, b):
             picked = v_pool[e][:].indirect(entries(b * N, SPANS[(e, b)] * N))
             if (e, b) in ON_SCALAR:
-                nc.scalar.activation(v_got[(e, b)][:], picked, ACT.Copy)
+                nc.scalar.activation(v_got[(e, b)][:].rearrange("p (u c h) -> p c u h", u=2, h=2), picked, ACT.Copy)
             else:
                 nc.vector.tensor_copy(v_got[(e, b)][:].rearrange("p (u c h) -> p c u h", u=2, h=2), picked)
 
         def pairs(e, b):
             first = b if (e, b) in SPANS else 0
             words = v_got[(e, first)][:].bitcast(F32)
-            order = "p (c u) -> p u c" if (e, first) in ON_SCALAR else "p (u c) -> p u c"
-            return words.rearrange(order, u=2)[:, :, (b - first) * P : (b - first + 1) * P]
+            return words.rearrange("p (u c) -> p u c", u=2)[:, :, (b - first) * P : (b - first + 1) * P]
 
         def turn(e, first, last):
             turned_v = bank(VALUE_BANK[(e, first)], [P, B, 2, P], "turned_v")
@@ -261,7 +260,8 @@ def tile_attend_gate_kernel(tc, qT, kT, vT, vs, og, offs, out):
         quantize_values(1, 0)
         lay(turned_last[1], LAST, 1, 2)
         gate_sigmoid(0)
-        gate_sigmoid(1)
+        for b in range(B):
+            nc.scalar.activation(sigmoid[1][:, b, :], gate[1][:, b, :], ACT.Sigmoid)
         for b in range(B):
             quantize_values(b, 1)
 

@@ -12,6 +12,8 @@ EB = DV // P
 HALF = DV // 2
 CODES = B * P
 ROW = 256
+RUN = 4
+EIGHT = 2 * RUN
 WORDS = 2 * CODES
 
 F32 = mybir.dt.float32
@@ -24,7 +26,7 @@ ACT = mybir.ActivationFunctionType
 ALU = mybir.AluOpType
 AXIS = mybir.AxisListType
 
-KEY_LOADS = [(0, 0, 1024, 1024), (0, 1024, 1024, 384), (1, 0, 1024, 512), (1, 1024, 768, 304), (1, 1792, 256, 88)]
+KEY_LOADS = [(0, 0, 1024), (0, 1024, 1024), (1, 0, 1024), (1, 1024, 768), (1, 1792, 256)]
 
 
 def tile_attend_gate_kernel(tc, qT, kT, vT, vs, og, offs, out):
@@ -50,7 +52,7 @@ def tile_attend_gate_kernel(tc, qT, kT, vT, vs, og, offs, out):
         nc.sync.dma_start(scale_row[:], vs[0:1, :])
         k_rows = kT.rearrange("(p a h) t -> p a h t", a=2, h=2)
         k_raw = []
-        for i, (a, first, width, cut) in enumerate(KEY_LOADS):
+        for i, (a, first, width) in enumerate(KEY_LOADS):
             if i == len(KEY_LOADS) - 1:
                 raw = room(1, [P, 2, width], F32, "k_raw_last")
             else:
@@ -77,19 +79,15 @@ def tile_attend_gate_kernel(tc, qT, kT, vT, vs, og, offs, out):
         ident = keep.tile([P, P], F32, name="ident")
         make_identity(nc, ident[:])
 
-        k_pair = [keep.tile([P, T, 2], BF16, name=f"k_pair{a}") for a in range(2)]
-        k_got = keep.tile([P, 2, B * N], U32, name="k_got")
+        k_windows = [keep.tile([P, T], U32, name=f"k_window{x}") for x in range(2)]
 
         def cast_keys(i):
-            a, first, width, cut = KEY_LOADS[i]
-            src = k_raw[i][:].rearrange("p h t -> p t h")
-            nc.scalar.activation(k_pair[a][:, first : first + cut, :], src[:, :cut, :], ACT.Copy)
-            if cut < width:
-                nc.vector.tensor_copy(k_pair[a][:, first + cut : first + width, :], src[:, cut:, :])
-
-        def gather_keys(a, first, count):
-            window = k_pair[a][:].rearrange("p t h -> p (t h)").bitcast(U32)
-            nc.vector.tensor_copy(k_got[:, a, first : first + count], window.indirect(entries(first, count)))
+            a, first, width = KEY_LOADS[i]
+            src = k_raw[i][:].rearrange("p h (m x i) -> p x m i h", x=2, i=RUN)
+            places = [w[:].bitcast(BF16).rearrange("p (m a i h) -> p a m i h", a=2, i=RUN, h=2) for w in k_windows]
+            runs = slice(first // EIGHT, (first + width) // EIGHT)
+            nc.vector.tensor_copy(places[0][:, a, runs], src[:, 0])
+            nc.scalar.activation(places[1][:, a, runs], src[:, 1], ACT.Copy)
 
         cast_keys(0)
         cast_keys(1)
@@ -106,29 +104,27 @@ def tile_attend_gate_kernel(tc, qT, kT, vT, vs, og, offs, out):
                 nc.tensor.transpose(turned[:, t, :], vs_row[:, b * N + t : (b + 1) * N : PACK], ident[:])
             vs_turned.append(turned)
 
-        gather_keys(0, 0, B * N)
         for i in range(2, len(KEY_LOADS)):
             cast_keys(i)
         vs_col = room(1, [P, B, PACK], F32, "vs_col")
         for b in range(B):
             nc.scalar.copy(vs_col[:, b, :], vs_turned[b][:, :, 0])
         k_words = keep.tile([P, B * N, 2], U32, align_bytes=64, name="k_words")
-        pieces = [(first, N // 2) for first in range(0, B * N, N // 2)]
-        for first, count in pieces:
-            gather_keys(1, first, count)
-        for first, count in pieces:
-            s = slice(first, first + count)
-            nc.scalar.copy(k_words[:, s, :], k_got[:, :, s].rearrange("p a n -> p n a"))
+        k_dealt = k_words[:].rearrange("p (m x i) a -> p x m a i", x=2, i=RUN)
+        for x in range(2):
+            nc.vector.tensor_copy(k_dealt[:, x], k_windows[x][:].indirect(lists[:]))
 
-        q_bf = keep.tile([P, B, NQ, PACK], BF16, align_bytes=64, name="q_bf")
+        q_bf = room(4, [P, B, NQ, PACK], BF16, "q_bf")
         q_codes = keep.tile([P, B * NQ], U32, align_bytes=64, name="q_codes")
         q_scales = keep.tile([P, B * NQ], U8, align_bytes=64, name="q_scales")
-        nc.gpsimd.tensor_scalar(q_bf[:], q_raw[:].rearrange("p b j q -> p b q j"), 1.0, 0.0, ALU.mult, ALU.add)
+        nc.scalar.copy(
+            q_bf[:].rearrange("p b (c i) j -> p b c j i", i=4), q_raw[:].rearrange("p b j (c i) -> p b c j i", i=4)
+        )
         nc.vector.quantize_mx(
             out=q_codes[:].bitcast(FP8X4), scales=q_scales[:], in_=q_bf[:].rearrange("p b q j -> p (b q j)")
         )
 
-        k_codes = keep.tile([P, B * N], U32, align_bytes=64, name="k_codes")
+        k_codes = room(4, [P, B * N], U32, "k_codes")
         k_scales = keep.tile([P, B * N], U8, align_bytes=64, name="k_scales")
         score = []
         for b in range(B):

@@ -26,7 +26,7 @@ ACT = mybir.ActivationFunctionType
 ALU = mybir.AluOpType
 AXIS = mybir.AxisListType
 
-KEY_LOADS = [(0, 0, 1024), (0, 1024, 1024), (1, 0, 1024), (1, 1024, 768), (1, 1792, 256)]
+KEY_LOADS = [(0, 0, 2048), (1, 0, 1536), (1, 1536, 512)]
 
 
 def tile_attend_gate_kernel(tc, qT, kT, vT, vs, og, offs, out):
@@ -50,6 +50,7 @@ def tile_attend_gate_kernel(tc, qT, kT, vT, vs, og, offs, out):
         lists = keep.tile([P, B * N // 16], U16, name="lists")
         scale_row = keep.tile([1, T], F32, align_bytes=ROW, name="scale_row")
         nc.sync.dma_start(scale_row[:], vs[0:1, :])
+        nc.sync.dma_start(lists[:], offs)
         k_rows = kT.rearrange("(p a h) t -> p a h t", a=2, h=2)
         k_raw = []
         for i, (a, first, width) in enumerate(KEY_LOADS):
@@ -59,9 +60,7 @@ def tile_attend_gate_kernel(tc, qT, kT, vT, vs, og, offs, out):
                 raw = keep.tile([P, 2, width], F32, align_bytes=ROW, name=f"k_raw{i}")
             nc.sync.dma_start(raw[:], k_rows[:, a, :, first : first + width])
             k_raw.append(raw)
-            if i == 0:
-                nc.sync.dma_start(lists[:], offs)
-        q_raw = keep.tile([P, B, PACK, NQ], F32, align_bytes=ROW, name="q_raw")
+        q_raw = room(4, [P, B, PACK, NQ], F32, "q_raw")
         nc.sync.dma_start(q_raw[:], qT.rearrange("b (p j) q -> p b j q", j=PACK))
         v_pool = [keep.tile([P, T], F32, align_bytes=ROW, name=f"v_pool{e}") for e in range(EB - 1)]
         v_pool.append(room(5, [P, T], F32, "v_pool3"))
@@ -114,7 +113,7 @@ def tile_attend_gate_kernel(tc, qT, kT, vT, vs, og, offs, out):
         for x in range(2):
             nc.vector.tensor_copy(k_dealt[:, x], k_windows[x][:].indirect(lists[:]))
 
-        q_bf = room(4, [P, B, NQ, PACK], BF16, "q_bf")
+        q_bf = keep.tile([P, B, NQ, PACK], BF16, align_bytes=64, name="q_bf")
         q_codes = keep.tile([P, B * NQ], U32, align_bytes=64, name="q_codes")
         q_scales = keep.tile([P, B * NQ], U8, align_bytes=64, name="q_scales")
         nc.scalar.copy(

@@ -49,7 +49,7 @@ def tile_attend_gate_kernel(tc, qT, kT, vT, vs, og, offs, out):
 
         lists = keep.tile([P, B * N // 16], U16, name="lists")
         scale_row = keep.tile([1, T], F32, align_bytes=ROW, name="scale_row")
-        nc.sync.dma_start(scale_row[:], vs[0:1, :])
+        nc.scalar.dma_start(scale_row[:], vs[0:1, :])
         nc.sync.dma_start(lists[:], offs)
         k_rows = kT.rearrange("(p a h) t -> p a h t", a=2, h=2)
         k_raw = []

from contextlib import ExitStack

import concourse.mybir as mybir
from concourse.masks import make_identity

B, N, T, D, DV, NQ = 2, 512, 2048, 512, 512, 128
FLOPS = 2 * B * NQ * N * (D + DV)

P = 128
PACK = 4
EB = DV // P
HALF = DV // 2
CODES = B * P
ROW = 256
RUN = 4
EIGHT = 2 * RUN
WORDS = 2 * CODES

F32 = mybir.dt.float32
BF16 = mybir.dt.bfloat16
U32 = mybir.dt.uint32
U16 = mybir.dt.uint16
U8 = mybir.dt.uint8
FP8X4 = mybir.dt.float8_e4m3fn_x4
ACT = mybir.ActivationFunctionType
ALU = mybir.AluOpType
AXIS = mybir.AxisListType

KEY_LOADS = [(0, 0, 2048), (1, 0, 1536), (1, 1536, 512)]


def tile_attend_gate_kernel(tc, qT, kT, vT, vs, og, offs, out):
    nc = tc.nc
    with ExitStack() as ctx:
        keep = ctx.enter_context(tc.tile_pool(name="keep", bufs=1))
        shared = ctx.enter_context(tc.tile_pool(name="shared", bufs=1))
        psum = ctx.enter_context(tc.psum_pool(name="psum", bufs=1))

        ROOM = T * 4

        def room(index, shape, dtype, name, skip=0):
            return shared.tile(shape, dtype, offset=index * ROOM + skip, align_bytes=ROW, name=name)

        def bank(index, shape, name):
            return psum.tile(shape, F32, tag=f"bank{index}", name=name)

        def entries(first, count):
            return lists[:, first // 16 : (first + count) // 16]

        lists = keep.tile([P, B * N // 16], U16, name="lists")
        scale_row = keep.tile([1, T], F32, align_bytes=ROW, name="scale_row")
        nc.scalar.dma_start(scale_row[:], vs[0:1, :])
        nc.sync.dma_start(lists[:], offs)
        k_rows = kT.rearrange("(p a h) t -> p a h t", a=2, h=2)
        k_raw = []
        for i, (a, first, width) in enumerate(KEY_LOADS):
            if i == len(KEY_LOADS) - 1:
                raw = room(1, [P, 2, width], F32, "k_raw_last")
            else:
                raw = keep.tile([P, 2, width], F32, align_bytes=ROW, name=f"k_raw{i}")
            nc.sync.dma_start(raw[:], k_rows[:, a, :, first : first + width])
            k_raw.append(raw)
        q_raw = room(4, [P, B, PACK, NQ], F32, "q_raw")
        nc.sync.dma_start(q_raw[:], qT.rearrange("b (p j) q -> p b j q", j=PACK))
        v_pool = [keep.tile([P, T], F32, align_bytes=ROW, name=f"v_pool{e}") for e in range(EB - 1)]
        v_pool.append(room(5, [P, T], F32, "v_pool3"))
        gate = [keep.tile([P, B, HALF], F32, align_bytes=ROW, name=f"gate{h}") for h in range(2)]
        gate_rows = og.rearrange("b q e -> q b e")
        for e in range(EB):
            nc.sync.dma_start(v_pool[e][:], vT[e * P : (e + 1) * P, :])
        nc.sync.dma_start(gate[0][:], gate_rows[:, :, :HALF])
        nc.sync.dma_start(gate[1][:], gate_rows[:, :, HALF:])

        minus_one = keep.tile([P, B], F32, name="minus_one")
        nc.gpsimd.memset(minus_one[:], -1.0)
        warm = keep.tile([P, 1], F32, name="warm")
        nc.scalar.activation(warm[:], minus_one[:, 0:1], ACT.Exp)
        ident = keep.tile([P, P], F32, name="ident")
        make_identity(nc, ident[:])

        k_windows = [keep.tile([P, T], U32, name=f"k_window{x}") for x in range(2)]

        def cast_keys(i):
            a, first, width = KEY_LOADS[i]
            src = k_raw[i][:].rearrange("p h (m x i) -> p x m i h", x=2, i=RUN)
            places = [w[:].bitcast(BF16).rearrange("p (m a i h) -> p a m i h", a=2, i=RUN, h=2) for w in k_windows]
            runs = slice(first // EIGHT, (first + width) // EIGHT)
            nc.vector.tensor_copy(places[0][:, a, runs], src[:, 0])
            nc.scalar.activation(places[1][:, a, runs], src[:, 1], ACT.Copy)

        cast_keys(0)
        cast_keys(1)

        scale_pool = keep.tile([P, T], F32, name="scale_pool")
        vs_row = keep.tile([P, B * N], F32, name="vs_row")
        nc.vector.memset(scale_pool[:], 0.0)
        nc.vector.tensor_copy(scale_pool[0:1, :], scale_row[:])
        nc.vector.tensor_copy(vs_row[:], scale_pool[:].indirect(lists[:]))
        vs_turned = []
        for b in range(B):
            turned = bank(b, [P, PACK, P], "vs_turned")
            for t in range(PACK):
                nc.tensor.transpose(turned[:, t, :], vs_row[:, b * N + t : (b + 1) * N : PACK], ident[:])
            vs_turned.append(turned)

        for i in range(2, len(KEY_LOADS)):
            cast_keys(i)
        vs_col = room(1, [P, B, PACK], F32, "vs_col")
        for b in range(B):
            nc.scalar.copy(vs_col[:, b, :], vs_turned[b][:, :, 0])
        k_words = keep.tile([P, B * N, 2], U32, align_bytes=64, name="k_words")
        k_dealt = k_words[:].rearrange("p (m x i) a -> p x m a i", x=2, i=RUN)
        for x in range(2):
            nc.vector.tensor_copy(k_dealt[:, x], k_windows[x][:].indirect(lists[:]))

        q_bf = keep.tile([P, B, NQ, PACK], BF16, align_bytes=64, name="q_bf")
        q_codes = keep.tile([P, B * NQ], U32, align_bytes=64, name="q_codes")
        q_scales = keep.tile([P, B * NQ], U8, align_bytes=64, name="q_scales")
        nc.scalar.copy(
            q_bf[:].rearrange("p b (c i) j -> p b c j i", i=4), q_raw[:].rearrange("p b j (c i) -> p b c j i", i=4)
        )
        nc.vector.quantize_mx(
            out=q_codes[:].bitcast(FP8X4), scales=q_scales[:], in_=q_bf[:].rearrange("p b q j -> p (b q j)")
        )

        k_codes = room(4, [P, B * N], U32, "k_codes")
        k_scales = keep.tile([P, B * N], U8, align_bytes=64, name="k_scales")
        score = []
        for b in range(B):
            s = slice(b * N, (b + 1) * N)
            qs = slice(b * NQ, (b + 1) * NQ)
            nc.vector.quantize_mx(
                out=k_codes[:, s].bitcast(FP8X4),
                scales=k_scales[:, s],
                in_=k_words[:, s, :].rearrange("p n a -> p (n a)").bitcast(BF16),
            )
            sums = bank(b, [P, N], "score")
            nc.tensor.matmul_mx(
                out=sums[:],
                lhsT=q_codes[:, qs].bitcast(FP8X4),
                lhsT_scale=q_scales[:, qs],
                rhs=k_codes[:, s].bitcast(FP8X4),
                rhs_scale=k_scales[:, s],
                start=True,
                stop=True,
            )
            score.append(sums)

        LAST = EB - 1
        ON_SCALAR = [(0, 0), (LAST, 1)]
        SPANS = {(0, 0): 2, (1, 0): 2, (2, 0): 2, (LAST, 0): 1, (LAST, 1): 1}
        HELD = {(LAST, 1): (3, 2048)}
        v_got = {}
        for (e, b), count in list(SPANS.items()):
            if (e, b) in HELD:
                v_got[(e, b)] = room(HELD[(e, b)][0], [P, count * N], BF16, f"v_got{e}{b}", skip=HELD[(e, b)][1])
            else:
                v_got[(e, b)] = keep.tile([P, count * N], BF16, name=f"v_got{e}{b}")
        v_words = [keep.tile([P, B, 2, P, 2], F32, align_bytes=64, name="v_words0")]
        VALUE_BANK = {(0, 0): 1, (1, 0): 0, (2, 0): 4, (LAST, 0): 5, (LAST, 1): 6}

        def gather_values(e, b):
            picked = v_pool[e][:].indirect(entries(b * N, SPANS[(e, b)] * N))
            if (e, b) in ON_SCALAR:
                nc.scalar.activation(v_got[(e, b)][:].rearrange("p (u c h) -> p c u h", u=2, h=2), picked, ACT.Copy)
            else:
                nc.vector.tensor_copy(v_got[(e, b)][:].rearrange("p (u c h) -> p c u h", u=2, h=2), picked)

        def pairs(e, b):
            first = b if (e, b) in SPANS else 0
            words = v_got[(e, first)][:].bitcast(F32)
            return words.rearrange("p (u c) -> p u c", u=2)[:, :, (b - first) * P : (b - first + 1) * P]

        def turn(e, first, last):
            turned_v = bank(VALUE_BANK[(e, first)], [P, B, 2, P], "turned_v")
            for b in range(first, last):
                for u in range(2):
                    nc.tensor.transpose(turned_v[:, b, u, :], pairs(e, b)[:, u, :], ident[:])
            return turned_v

        def lay(turned_v, e, first, last, copy=nc.scalar.copy):
            copy(
                v_words[e // 2][:, first:last, e % 2, :, :],
                turned_v[:, first:last, :, :].rearrange("p b u e -> p b e u"),
            )

        def turn_values(e, first, last):
            lay(turn(e, first, last), e, first, last)

        gather_values(0, 0)

        minus = room(2, [P, B], F32, "minus")
        total = keep.tile([P, B], F32, name="total")
        weight = [keep.tile([P, PACK, P], F32, name=f"weight{b}") for b in range(B)]
        for b in range(B):
            nc.vector.tensor_reduce(minus[:, b : b + 1], score[b][:], axis=AXIS.X, op=ALU.max, negate=True)
            nc.scalar.activation(
                weight[b][:],
                score[b][:].rearrange("p (c t) -> p t c", t=PACK),
                ACT.Exp,
                bias=minus[:, b : b + 1],
                accum_out=total[:, b : b + 1],
            )
        warm_sigmoid = room(2, [P, 1], F32, "warm_sigmoid")
        nc.scalar.activation(warm_sigmoid[:], minus_one[:, 0:1], ACT.Sigmoid)
        gather_values(1, 0)

        inverse = keep.tile([P, B], F32, name="inverse")
        w_turned = [bank(2 + b, [P, PACK, P], "w_turned") for b in range(B)]
        for b in range(B):
            for t in range(PACK):
                nc.tensor.transpose(w_turned[b][:, t, :], weight[b][:, t, :], ident[:])
        turn_values(0, 0, B)
        w_bf = keep.tile([P, B, NQ, PACK], BF16, align_bytes=64, name="w_bf")
        for b in range(B):
            nc.vector.tensor_tensor(
                w_bf[:, b, :, :].rearrange("p (c i) t -> p c t i", i=4),
                w_turned[b][:].rearrange("p t (c i) -> p c t i", i=4),
                vs_col[:, b, :].unsqueeze(1).unsqueeze(3).to_broadcast([P, NQ // 4, PACK, 4]),
                ALU.mult,
            )
        nc.gpsimd.tensor_tensor(inverse[:], total[:], minus_one[:], ALU.pow)
        turn_values(1, 0, B)
        gather_values(2, 0)
        turned_two = turn(2, 0, B)
        for b in range(B):
            gather_values(LAST, b)
        turned_last = [turn(LAST, b, b + 1) for b in range(B)]
        v_words.append(room(5, [P, B, 2, P, 2], F32, "v_words1", skip=(EB + 1) * CODES * 4))
        lay(turned_two, 2, 0, B)

        sigmoid = [room(3, [P, B, HALF], F32, "sigmoid0", skip=512), room(3, [P, B, HALF], F32, "sigmoid1", skip=2560)]

        def gate_sigmoid(h):
            nc.scalar.activation(sigmoid[h][:], gate[h][:], ACT.Sigmoid)

        w_codes = room(5, [P, CODES], U32, "w_codes")
        w_scales = keep.tile([P, CODES], U8, align_bytes=64, name="w_scales")
        v_codes = room(5, [P, EB * CODES], U32, "v_codes", skip=CODES * 4)
        v_scales = keep.tile([P, EB * CODES], U8, align_bytes=64, name="v_scales")

        def quantize_values(b, h):
            cols = slice(b * DV + h * HALF, b * DV + (h + 1) * HALF)
            nc.vector.quantize_mx(
                out=v_codes[:, cols].bitcast(FP8X4),
                scales=v_scales[:, cols],
                in_=v_words[h][:, b, :, :, :].rearrange("p f e u -> p (f e u)").bitcast(BF16),
            )

        nc.vector.quantize_mx(
            out=w_codes[:].bitcast(FP8X4), scales=w_scales[:], in_=w_bf[:].rearrange("p b q t -> p (b q t)")
        )
        quantize_values(0, 0)
        lay(turned_last[0], LAST, 0, 1, nc.vector.tensor_copy)
        quantize_values(1, 0)
        lay(turned_last[1], LAST, 1, 2)
        gate_sigmoid(0)
        for b in range(B):
            nc.scalar.activation(sigmoid[1][:, b, :], gate[1][:, b, :], ACT.Sigmoid)
        for b in range(B):
            quantize_values(b, 1)

        res = keep.tile([P, B, DV], F32, align_bytes=ROW, name="res")

        def attend(b, first, last):
            y = bank(first + b, [P, (last - first) * P], "y")
            cols = slice(b * P, (b + 1) * P)
            v_cols = slice(b * DV + first * P, b * DV + last * P)
            nc.tensor.matmul_mx(
                out=y[:],
                lhsT=w_codes[:, cols].bitcast(FP8X4),
                lhsT_scale=w_scales[:, cols],
                rhs=v_codes[:, v_cols].bitcast(FP8X4),
                rhs_scale=v_scales[:, v_cols],
                start=True,
                stop=True,
            )
            es = slice(first * P, last * P)
            gs = slice(first * P % HALF, (last * P - 1) % HALF + 1)
            nc.vector.scalar_tensor_tensor(
                res[:, b, es], y[:], inverse[:, b : b + 1], sigmoid[first * P // HALF][:, b, gs], ALU.mult, ALU.mult
            )
            nc.sync.dma_start(out[b, :, es], res[:, b, es])

        for first, last in [(0, 2), (2, 4)]:
            for b in range(B):
                attend(b, first, last)
